import numpy as np
import ml_dtypes


def mxq(x, axis, fmt="e4m3"):
    dtype, down = {"e4m3": (ml_dtypes.float8_e4m3fn, 7), "e5m2": (ml_dtypes.float8_e5m2, 14)}[fmt]
    v = np.moveaxis(np.asarray(x, np.float32).astype(ml_dtypes.bfloat16).astype(np.float64), axis, -1)
    blocks = v.reshape(v.shape[:-1] + (-1, 32))
    amax = np.abs(blocks).max(-1, keepdims=True)
    byte = np.maximum(np.where(amax > 0, np.frexp(amax)[1] - 1 + 127, 0) - down, 1)
    scale = np.exp2(byte - 127.0)
    codes = (blocks / scale).astype(np.float32).astype(dtype).astype(np.float64)
    return np.moveaxis((codes * scale).reshape(v.shape), -1, axis)


WIDE = False


def mx_kscale(k):
    if not WIDE:
        return np.ones(k)
    levels = np.array([10, -10, 5, -5, 0])
    if k % 512:
        return np.exp2(np.random.permutation(np.resize(levels, k // 32))).repeat(32)
    a = np.empty((k // 512, 16))
    for p in range(k // 512):
        a[p, :8] = np.random.permutation(np.resize(levels, 8))
        for g in range(8):
            far = levels[np.abs(levels - a[p, g]) >= 10]
            a[p, g + 8] = far[np.random.randint(len(far))]
    return np.exp2(a.ravel()).repeat(32)


def f64(x):
    return np.asarray(x).astype(np.float64)


def striped(idx):
    return np.tile(idx.reshape(-1, 16).T, (8, 1)).astype(np.uint16)


def unstriped(offs):
    return offs[:16].T.reshape(-1).astype(np.int64)


def pack_weight(w):
    k, n = w.shape
    w = f64(np.asarray(w, np.float32).astype(ml_dtypes.bfloat16)).reshape(k // 32, 32, n)
    amax = np.abs(w).max(1)
    byte = np.clip(np.where(amax > 0, np.frexp(amax)[1] - 1 + 127 - 7, 1), 1, 254)
    scaled = (w * np.exp2(127.0 - byte)[:, None, :]).reshape(k, n).astype(np.float32)
    words = np.ascontiguousarray(scaled.reshape(k // 512, 128, 4, n).transpose(0, 1, 3, 2)).astype(ml_dtypes.float8_e4m3fn).view(np.uint8)
    return words, np.ascontiguousarray(byte.astype(np.uint8).reshape(k // 512, 16, n))


def unpack_weight(words, scales):
    g, p, n, _ = words.shape
    vals = np.ascontiguousarray(words).view(ml_dtypes.float8_e4m3fn).astype(np.float64) * np.repeat(np.exp2(scales.astype(np.float64) - 127.0), 8, axis=1)[..., None]
    return vals.transpose(0, 1, 3, 2).reshape(g * 512, n)


K, T, S, H, N = 512, 2048, 1024, 512, 128
P = 2 ** 7


def setup_inputs():
    n = np.random.standard_normal
    s = mx_kscale(K)[:, None]
    u = mx_kscale(H)
    packed_xT = pack_weight(n((K, T)) * s)
    packed_w2 = pack_weight(n((H, N)) / np.sqrt(H) / u[:, None])
    return {
        "x_words": packed_xT[0],
        "x_scales": packed_xT[1],
        "w1": (n((K, H)) / np.sqrt(K) / s * u).astype(np.float32),
        "w2_words": packed_w2[0],
        "w2_scales": packed_w2[1],
        "lam": np.tile(np.random.uniform(0.1, 0.9, S), (P, 1)).astype(np.float32),
        "mu": np.tile(np.random.uniform(0.1, 0.9, S), (P, 1)).astype(np.float32),
        "offs": striped(np.random.permutation(T)[:S]),
        "pos1": striped(np.random.permutation(S)),
    }


def reference(x_words, x_scales, w1, w2_words, w2_scales, lam, mu, offs, pos1):
    xq = unpack_weight(x_words, x_scales)[:, unstriped(offs)]
    h = mxq(f64(w1), 0, "e4m3").T @ xq
    z = h * f64(lam)[:1] + h[:, unstriped(pos1)] * f64(mu)[:1]
    return unpack_weight(w2_words, w2_scales).T @ mxq(z, 0, "e4m3")

@@ -1,0 +1,194 @@
+from contextlib import ExitStack
+
+import concourse.mybir as mybir
+from concourse.masks import make_identity
+
+K, T, S, H, N = 512, 2048, 1024, 512, 128
+FLOPS = 2 * K * H * S + 2 * H * N * S
+BYTES = K * T + K * T // 32 + 4 * K * H + H * N + H * N // 32 + 2 * 4 * S + 2 * 2 * 128 * (S // 16) + 4 * N * S
+
+F32 = mybir.dt.float32
+BF16 = mybir.dt.bfloat16
+I32 = mybir.dt.int32
+U32 = mybir.dt.uint32
+U16 = mybir.dt.uint16
+U8 = mybir.dt.uint8
+FP8X4 = mybir.dt.float8_e4m3fn_x4
+MULT = mybir.AluOpType.mult
+ADD = mybir.AluOpType.add
+COPY = mybir.ActivationFunctionType.Copy
+
+P = 128
+HALF = 512
+BLOCKS = S // P
+TILES = 4
+COL0 = [0, 256, 128, 384]
+UNITS = [(0, 1), (2, 3), (4, 5), (6,), (7,)]
+
+
+def tile_picked_mixup_none_p_kernel(
+    tc, x_words, x_scales, w1, w2_words, w2_scales, lam, mu, offs, pos1, out
+):
+    nc = tc.nc
+    with ExitStack() as ctx:
+        keep = ctx.enter_context(tc.tile_pool(name="keep", bufs=1))
+        psum = ctx.enter_context(tc.psum_pool(name="psum", bufs=1))
+
+        def bank(b):
+            return psum.tile([P, HALF], F32, name="bank%d" % b, tag="bank%d" % b)
+
+        def entries(lst, j0, n):
+            return lst[:, j0 // 16 : (j0 + n) // 16]
+
+        offs_sb = keep.tile([P, S // 16], U16, name="offs_sb")
+        pos_sb = keep.tile([P, S // 16], U16, name="pos_sb")
+        xs = keep.tile([P, T], U8, name="xs", align_bytes=64)
+        xw = keep.tile([P, T], I32, name="xw", align_bytes=64)
+        shares = keep.tile([P, P], F32, name="shares")
+        w2w = keep.tile([P, N], I32, name="w2w", align_bytes=64)
+        w2s = keep.tile([P, N], U8, name="w2s", align_bytes=64)
+        ident = keep.tile([P, P], F32, name="ident")
+
+        nc.vector.memset(xs[:].bitcast(I32), 0)
+        nc.vector.memset(w2s[:].bitcast(I32), 0)
+        make_identity(nc, ident[:])
+
+        nc.sync.dma_start(offs_sb[:], offs)
+        nc.sync.dma_start(shares[0:64, :], lam[0:8, :].rearrange("r (b c) -> (r b) c", c=P))
+        nc.sync.dma_start(shares[64:128, :], mu[0:8, :].rearrange("r (b c) -> (r b) c", c=P))
+        for q in range(4):
+            nc.sync.dma_start(xs[32 * q : 32 * q + 4, :].bitcast(I32), x_scales[0, 4 * q : 4 * q + 4, :].bitcast(I32))
+        nc.sync.dma_start(xw[:], x_words[0].rearrange("p n t -> p (n t)").bitcast(I32))
+        w_raw = []
+        for hq in range(2):
+            raw = keep.tile([P, 4, 256], F32, name="w_raw%d" % hq)
+            nc.sync.dma_start(raw[:], w1[:, 256 * hq : 256 * hq + 256].rearrange("(p j) c -> p j c", j=4))
+            w_raw.append(raw)
+        nc.sync.dma_start(pos_sb[:], pos1)
+        nc.sync.dma_start(w2w[:], w2_words[0].rearrange("p n t -> p (n t)").bitcast(I32))
+        for q in range(4):
+            nc.sync.dma_start(w2s[32 * q : 32 * q + 4, :].bitcast(I32), w2_scales[0, 4 * q : 4 * q + 4, :].bitcast(I32))
+
+        turned = bank(BLOCKS - 1)
+        nc.tensor.transpose(turned[:, 0:P], shares[:], ident[:])
+        lam_t = keep.tile([P, BLOCKS], F32, name="lam_t", tag="late")
+        mu_t = keep.tile([P, BLOCKS], F32, name="mu_t")
+        nc.scalar.copy(lam_t[:], turned[:, 0:BLOCKS])
+        nc.scalar.copy(mu_t[:], turned[:, 64 : 64 + BLOCKS])
+
+        xgs = keep.tile([P, S], U8, name="xgs", align_bytes=64)
+        nc.vector.tensor_copy(xgs[:], xs[:].indirect(offs_sb[:]))
+        xg = []
+        for s in range(2):
+            g = keep.tile([P, HALF], U32, name="xg%d" % s, align_bytes=64)
+            nc.vector.tensor_copy(g[:], xw[:].bitcast(U32).indirect(entries(offs_sb, s * HALF, HALF)))
+            xg.append(g)
+
+        w_codes, w_scales = [], []
+        for t in range(TILES):
+            hq, u = divmod(t, 2)
+            grouped = keep.tile([P, 64, 2, 4], BF16, name="w_grouped%d" % t, align_bytes=64)
+            nc.scalar.copy(grouped[:], w_raw[hq][:].rearrange("p j (q u e) -> p u q e j", u=2, e=2)[:, u])
+            codes = keep.tile([P, P], U32, name="w_codes%d" % t, align_bytes=64)
+            scales = keep.tile([P, P], U8, name="w_scales%d" % t, align_bytes=64)
+            nc.vector.quantize_mx(
+                out=codes[:].bitcast(FP8X4), scales=scales[:], in_=grouped[:].rearrange("p q e j -> p (q e j)")
+            )
+            w_codes.append(codes)
+            w_scales.append(scales)
+
+        h = []
+        for t in range(TILES):
+            h_t = keep.tile([P, S], F32, name="h%d" % t)
+            for s in range(2):
+                acc = bank(2 * t + s)
+                nc.tensor.matmul_mx(
+                    out=acc[:],
+                    lhsT=w_codes[t][:].bitcast(FP8X4),
+                    lhsT_scale=w_scales[t][:],
+                    rhs=xg[s][:].bitcast(FP8X4),
+                    rhs_scale=xgs[:, s * HALF : (s + 1) * HALF],
+                    start=True,
+                    stop=True,
+                )
+                if (t, s) == (0, 1):
+                    nc.vector.tensor_copy(h_t[:, s * HALF : (s + 1) * HALF], acc[:])
+                else:
+                    nc.scalar.copy(h_t[:, s * HALF : (s + 1) * HALF], acc[:])
+            h.append(h_t)
+
+        def gather(dst, s, t):
+            cut = HALF // 2 if t == TILES - 1 else HALF
+            for c0 in range(0, HALF, cut):
+                nc.vector.tensor_copy(dst[:, c0 : c0 + cut], h[t][:].indirect(entries(pos_sb, s * HALF + c0, cut)))
+
+        partner = {}
+        for s, t in [(0, 0), (1, 0), (0, 1), (0, 2), (0, 3)]:
+            g = keep.tile([P, HALF], F32, name="partner%d%d" % (s, t))
+            gather(g[:], s, t)
+            partner[(s, t)] = g[:]
+
+        own = []
+        for b in range(BLOCKS):
+            turned = bank(b)
+            for t in range(TILES):
+                nc.tensor.transpose(turned[:, COL0[t] : COL0[t] + P], h[t][:, b * P : (b + 1) * P], ident[:])
+            a = keep.tile([P, H], F32, name="own%d" % b, tag="own%d" % b)
+            nc.scalar.activation(a[:], turned[:], COPY, scale=lam_t[:, b : b + 1])
+            own.append(a)
+
+        z_t = []
+
+        def mix(b):
+            s, c0 = b // 4, (b % 4) * P
+            turned = bank(b)
+            for t in range(TILES):
+                nc.tensor.transpose(turned[:, COL0[t] : COL0[t] + P], partner[(s, t)][:, c0 : c0 + P], ident[:])
+            z = keep.tile([P, H], BF16, name="z%d" % b)
+            nc.vector.scalar_tensor_tensor(z[:], turned[:], mu_t[:, b : b + 1], own[b][:], MULT, ADD)
+            z_t.append(z)
+
+        mix(0)
+        mix(1)
+        g = keep.tile([P, HALF], F32, name="partner11", tag="own1")
+        gather(g[:], 1, 1)
+        partner[(1, 1)] = g[:]
+        mix(2)
+        mix(3)
+        late = keep.tile([P, 2, HALF], F32, name="partner_late", tag="late")
+        for t in (2, 3):
+            gather(late[:, t - 2, :], 1, t)
+            partner[(1, t)] = late[:, t - 2, :]
+        for b in range(4, BLOCKS):
+            mix(b)
+
+        for unit in UNITS:
+            n = len(unit) * P
+            j0 = unit[0] * P
+            grouped = keep.tile([P, n, 2], F32, name="z_grouped%d" % unit[0], align_bytes=64)
+            for k, b in enumerate(unit):
+                turned = bank(b)
+                words = z_t[b][:].bitcast(F32)
+                for u in range(2):
+                    nc.tensor.transpose(turned[:, u * P : (u + 1) * P], words[:, u * P : (u + 1) * P], ident[:])
+                nc.scalar.copy(grouped[:, k * P : (k + 1) * P, :], turned[:, 0 : 2 * P].rearrange("p (u j) -> p j u", u=2))
+            codes = keep.tile([P, n], U32, name="z_codes%d" % unit[0], align_bytes=64)
+            scales = keep.tile([P, n], U8, name="z_scales%d" % unit[0], align_bytes=64)
+            nc.vector.quantize_mx(
+                out=codes[:].bitcast(FP8X4),
+                scales=scales[:],
+                in_=grouped[:].rearrange("p j u -> p (j u)").bitcast(BF16),
+            )
+            acc = bank(unit[-1])
+            nc.tensor.matmul_mx(
+                out=acc[:, 0:n],
+                lhsT=w2w[:].bitcast(FP8X4),
+                lhsT_scale=w2s[:],
+                rhs=codes[:].bitcast(FP8X4),
+                rhs_scale=scales[:],
+                start=True,
+                stop=True,
+            )
+            res = keep.tile([P, n], F32, name="res%d" % unit[0])
+            nc.scalar.copy(res[:], acc[:, 0:n])
+            nc.sync.dma_start(out[:, j0 : j0 + n], res[:])

@@ -22,7 +22,8 @@ P = 128
 HALF = 512
 BLOCKS = S // P
 TILES = 4
-COL0 = [0, 256, 128, 384]
+X_PIECES = [(0, 512), (512, 256), (768, 256)]
+CODES_TAG = {0: "z_codes0", 2: "own6", 4: "own7", 6: "z_codes6", 7: "z_codes7"}
 UNITS = [(0, 1), (2, 3), (4, 5), (6,), (7,)]
 
 
@@ -40,10 +41,14 @@ def tile_picked_mixup_none_p_kernel(
         def entries(lst, j0, n):
             return lst[:, j0 // 16 : (j0 + n) // 16]
 
+        def turn(dst_bank, t, src, start=True, stop=True):
+            dst = dst_bank[:].rearrange("p (u t x) -> p u t x", u=2, t=TILES)[:, :, t, :]
+            nc.tensor.matmul(dst, src, ident[:], start=start, stop=stop, is_transpose=True)
+
         offs_sb = keep.tile([P, S // 16], U16, name="offs_sb")
         pos_sb = keep.tile([P, S // 16], U16, name="pos_sb")
         xs = keep.tile([P, T], U8, name="xs", align_bytes=64)
-        xw = keep.tile([P, T], I32, name="xw", align_bytes=64)
+        xw = keep.tile([P, T], I32, name="xw", tag="xw", align_bytes=64)
         shares = keep.tile([P, P], F32, name="shares")
         w2w = keep.tile([P, N], I32, name="w2w", align_bytes=64)
         w2s = keep.tile([P, N], U8, name="w2s", align_bytes=64)
@@ -60,16 +65,17 @@ def tile_picked_mixup_none_p_kernel(
             nc.sync.dma_start(xs[32 * q : 32 * q + 4, :].bitcast(I32), x_scales[0, 4 * q : 4 * q + 4, :].bitcast(I32))
         nc.sync.dma_start(xw[:], x_words[0].rearrange("p n t -> p (n t)").bitcast(I32))
         w_raw = []
-        for hq in range(2):
-            raw = keep.tile([P, 4, 256], F32, name="w_raw%d" % hq)
-            nc.sync.dma_start(raw[:], w1[:, 256 * hq : 256 * hq + 256].rearrange("(p j) c -> p j c", j=4))
-            w_raw.append(raw)
+        for c0, c1 in [(0, 128), (128, 256), (256, 512)]:
+            raw = keep.tile([P, 4, c1 - c0], F32, name="w_raw%d" % c0)
+            nc.sync.dma_start(raw[:], w1[:, c0:c1].rearrange("(p j) c -> p j c", j=4))
+            for c in range(0, c1 - c0, P):
+                w_raw.append(raw[:, :, c : c + P].rearrange("p j (q u e) -> p u q e j", u=2, e=2))
         nc.sync.dma_start(pos_sb[:], pos1)
         nc.sync.dma_start(w2w[:], w2_words[0].rearrange("p n t -> p (n t)").bitcast(I32))
         for q in range(4):
             nc.sync.dma_start(w2s[32 * q : 32 * q + 4, :].bitcast(I32), w2_scales[0, 4 * q : 4 * q + 4, :].bitcast(I32))
 
-        turned = bank(BLOCKS - 1)
+        turned = bank(7)
         nc.tensor.transpose(turned[:, 0:P], shares[:], ident[:])
         lam_t = keep.tile([P, BLOCKS], F32, name="lam_t", tag="late")
         mu_t = keep.tile([P, BLOCKS], F32, name="mu_t")
@@ -78,63 +84,101 @@ def tile_picked_mixup_none_p_kernel(
 
         xgs = keep.tile([P, S], U8, name="xgs", align_bytes=64)
         nc.vector.tensor_copy(xgs[:], xs[:].indirect(offs_sb[:]))
-        xg = []
-        for s in range(2):
-            g = keep.tile([P, HALF], U32, name="xg%d" % s, align_bytes=64)
-            nc.vector.tensor_copy(g[:], xw[:].bitcast(U32).indirect(entries(offs_sb, s * HALF, HALF)))
-            xg.append(g)
 
-        w_codes, w_scales = [], []
-        for t in range(TILES):
-            hq, u = divmod(t, 2)
-            grouped = keep.tile([P, 64, 2, 4], BF16, name="w_grouped%d" % t, align_bytes=64)
-            nc.scalar.copy(grouped[:], w_raw[hq][:].rearrange("p j (q u e) -> p u q e j", u=2, e=2)[:, u])
-            codes = keep.tile([P, P], U32, name="w_codes%d" % t, align_bytes=64)
-            scales = keep.tile([P, P], U8, name="w_scales%d" % t, align_bytes=64)
+        w_codes = keep.tile([P, H], U32, name="w_codes", align_bytes=64)
+        w_scales = keep.tile([P, H], U8, name="w_scales", align_bytes=64)
+
+        def quantise_w(t):
+            tag = "xw" if t == TILES - 1 else "w_grouped%d" % t
+            grouped = keep.tile([P, 2, 32, 2, 4], BF16, name="w_grouped%d" % t, tag=tag, align_bytes=64)
+            if t == TILES - 1:
+                nc.vector.tensor_copy(grouped[:], w_raw[t])
+            else:
+                nc.scalar.copy(grouped[:], w_raw[t])
             nc.vector.quantize_mx(
-                out=codes[:].bitcast(FP8X4), scales=scales[:], in_=grouped[:].rearrange("p q e j -> p (q e j)")
+                out=w_codes[:, t * P : (t + 1) * P].bitcast(FP8X4),
+                scales=w_scales[:, t * P : (t + 1) * P],
+                in_=grouped[:].rearrange("p u q e j -> p (u q e j)"),
             )
-            w_codes.append(codes)
-            w_scales.append(scales)
 
-        h = []
-        for t in range(TILES):
-            h_t = keep.tile([P, S], F32, name="h%d" % t)
-            for s in range(2):
-                acc = bank(2 * t + s)
+        quantise_w(0)
+        xg = keep.tile([P, 768], U32, name="xg", align_bytes=64)
+        xg_end = keep.tile([P, 256], U32, name="xg_end", tag="w_grouped0", align_bytes=64)
+
+        def picked(j0, n):
+            return xg[:, j0 : j0 + n] if j0 < 768 else xg_end[:]
+
+        for j0, n in X_PIECES:
+            nc.vector.tensor_copy(picked(j0, n), xw[:].bitcast(U32).indirect(entries(offs_sb, j0, n)))
+        quantise_w(1)
+
+        def first_product(t, b, pieces, on_vector):
+            acc = bank(b)
+            j_first = pieces[0][0]
+            for j0, n in pieces:
                 nc.tensor.matmul_mx(
-                    out=acc[:],
-                    lhsT=w_codes[t][:].bitcast(FP8X4),
-                    lhsT_scale=w_scales[t][:],
-                    rhs=xg[s][:].bitcast(FP8X4),
-                    rhs_scale=xgs[:, s * HALF : (s + 1) * HALF],
+                    out=acc[:, j0 - j_first : j0 - j_first + n],
+                    lhsT=w_codes[:, t * P : (t + 1) * P].bitcast(FP8X4),
+                    lhsT_scale=w_scales[:, t * P : (t + 1) * P],
+                    rhs=picked(j0, n).bitcast(FP8X4),
+                    rhs_scale=xgs[:, j0 : j0 + n],
                     start=True,
                     stop=True,
                 )
-                if (t, s) == (0, 1):
-                    nc.vector.tensor_copy(h_t[:, s * HALF : (s + 1) * HALF], acc[:])
-                else:
-                    nc.scalar.copy(h_t[:, s * HALF : (s + 1) * HALF], acc[:])
-            h.append(h_t)
+            width = sum(n for j0, n in pieces)
+            if on_vector:
+                nc.vector.tensor_copy(h[t][:, j_first : j_first + width], acc[:, 0:width])
+            else:
+                nc.scalar.copy(h[t][:, j_first : j_first + width], acc[:, 0:width])
 
-        def gather(dst, s, t):
+        h = [keep.tile([P, S], F32, name="h%d" % t) for t in range(TILES)]
+        first_product(0, 0, X_PIECES[0:1], False)
+        first_product(0, 1, X_PIECES[1:2], False)
+        first_product(0, 7, X_PIECES[2:3], False)
+        for t in range(1, TILES):
+            if t + 1 < TILES:
+                quantise_w(t + 1)
+            first_product(t, 2 * t, X_PIECES[0:1], False)
+            first_product(t, 2 * t + 1, X_PIECES[1:3], False)
+
+        def gather(dst, t, j0, n):
+            nc.vector.tensor_copy(dst, h[t][:].indirect(entries(pos_sb, j0, n)))
+
+        def gather_half(dst, s, t):
             cut = HALF // 2 if t == TILES - 1 else HALF
             for c0 in range(0, HALF, cut):
-                nc.vector.tensor_copy(dst[:, c0 : c0 + cut], h[t][:].indirect(entries(pos_sb, s * HALF + c0, cut)))
+                gather(dst[:, c0 : c0 + cut], t, s * HALF + c0, cut)
 
         partner = {}
         for s, t in [(0, 0), (1, 0), (0, 1), (0, 2), (0, 3)]:
             g = keep.tile([P, HALF], F32, name="partner%d%d" % (s, t))
-            gather(g[:], s, t)
+            gather_half(g[:], s, t)
             partner[(s, t)] = g[:]
 
         own = []
         for b in range(BLOCKS):
             turned = bank(b)
-            for t in range(TILES):
-                nc.tensor.transpose(turned[:, COL0[t] : COL0[t] + P], h[t][:, b * P : (b + 1) * P], ident[:])
-            a = keep.tile([P, H], F32, name="own%d" % b, tag="own%d" % b)
-            nc.scalar.activation(a[:], turned[:], COPY, scale=lam_t[:, b : b + 1])
+            a = keep.tile([P, H], F32, name="own%d" % b, tag="own%d" % b, align_bytes=64)
+            if b < BLOCKS - 2:
+                for t in range(TILES):
+                    turn(turned, t, h[t][:, b * P : (b + 1) * P])
+                nc.scalar.activation(a[:], turned[:], COPY, scale=lam_t[:, b : b + 1])
+            else:
+                nc.tensor.matmul_mx(
+                    out=turned[:],
+                    lhsT=xg_end[:, b * P - 768 : (b + 1) * P - 768].bitcast(FP8X4),
+                    lhsT_scale=xgs[:, b * P : (b + 1) * P],
+                    rhs=w_codes[:].bitcast(FP8X4),
+                    rhs_scale=w_scales[:],
+                    start=True,
+                    stop=True,
+                )
+                nc.scalar.activation(
+                    a[:].rearrange("p (u t x) -> p u t x", u=2, t=TILES),
+                    turned[:].rearrange("p (t u x) -> p u t x", u=2, t=TILES),
+                    COPY,
+                    scale=lam_t[:, b : b + 1],
+                )
             own.append(a)
 
         z_t = []
@@ -143,36 +187,30 @@ def tile_picked_mixup_none_p_kernel(
             s, c0 = b // 4, (b % 4) * P
             turned = bank(b)
             for t in range(TILES):
-                nc.tensor.transpose(turned[:, COL0[t] : COL0[t] + P], partner[(s, t)][:, c0 : c0 + P], ident[:])
+                turn(turned, t, partner[(s, t)][:, c0 : c0 + P])
             z = keep.tile([P, H], BF16, name="z%d" % b)
             nc.vector.scalar_tensor_tensor(z[:], turned[:], mu_t[:, b : b + 1], own[b][:], MULT, ADD)
             z_t.append(z)
 
-        mix(0)
-        mix(1)
-        g = keep.tile([P, HALF], F32, name="partner11", tag="own1")
-        gather(g[:], 1, 1)
-        partner[(1, 1)] = g[:]
-        mix(2)
-        mix(3)
-        late = keep.tile([P, 2, HALF], F32, name="partner_late", tag="late")
-        for t in (2, 3):
-            gather(late[:, t - 2, :], 1, t)
-            partner[(1, t)] = late[:, t - 2, :]
-        for b in range(4, BLOCKS):
-            mix(b)
-
+        z_grouped = {}
         for unit in UNITS:
-            n = len(unit) * P
-            j0 = unit[0] * P
-            grouped = keep.tile([P, n, 2], F32, name="z_grouped%d" % unit[0], align_bytes=64)
+            z_grouped[unit] = keep.tile([P, len(unit) * P, 2], F32, name="z_grouped%d" % unit[0], align_bytes=64)
+
+        def turn_back(unit):
             for k, b in enumerate(unit):
                 turned = bank(b)
                 words = z_t[b][:].bitcast(F32)
                 for u in range(2):
                     nc.tensor.transpose(turned[:, u * P : (u + 1) * P], words[:, u * P : (u + 1) * P], ident[:])
-                nc.scalar.copy(grouped[:, k * P : (k + 1) * P, :], turned[:, 0 : 2 * P].rearrange("p (u j) -> p j u", u=2))
-            codes = keep.tile([P, n], U32, name="z_codes%d" % unit[0], align_bytes=64)
+                nc.scalar.copy(
+                    z_grouped[unit][:, k * P : (k + 1) * P, :], turned[:, 0 : 2 * P].rearrange("p (u j) -> p j u", u=2)
+                )
+
+        def finish(unit):
+            n = len(unit) * P
+            j0 = unit[0] * P
+            grouped = z_grouped[unit]
+            codes = keep.tile([P, n], U32, name="z_codes%d" % unit[0], tag=CODES_TAG[unit[0]], align_bytes=64)
             scales = keep.tile([P, n], U8, name="z_scales%d" % unit[0], align_bytes=64)
             nc.vector.quantize_mx(
                 out=codes[:].bitcast(FP8X4),
@@ -192,3 +230,24 @@ def tile_picked_mixup_none_p_kernel(
             res = keep.tile([P, n], F32, name="res%d" % unit[0])
             nc.scalar.copy(res[:], acc[:, 0:n])
             nc.sync.dma_start(out[:, j0 : j0 + n], res[:])
+
+        mix(0)
+        mix(1)
+        g = keep.tile([P, HALF], F32, name="partner11", tag="own1", align_bytes=64)
+        gather_half(g[:], 1, 1)
+        partner[(1, 1)] = g[:]
+        mix(2)
+        mix(3)
+        late = keep.tile([P, 2, HALF], F32, name="partner_late", tag="late")
+        for t in (2, 3):
+            gather_half(late[:, t - 2, :], 1, t)
+            partner[(1, t)] = late[:, t - 2, :]
+        turn_back(UNITS[0])
+        turn_back(UNITS[1])
+        finish(UNITS[0])
+        for b in range(4, BLOCKS):
+            mix(b)
+        for unit in UNITS[2:]:
+            turn_back(unit)
+        for unit in UNITS[1:]:
+            finish(unit)

@@ -23,7 +23,10 @@ HALF = 512
 BLOCKS = S // P
 TILES = 4
 X_PIECES = [(0, 512), (512, 256), (768, 256)]
-CODES_TAG = {0: "z_codes0", 2: "own6", 4: "own7", 6: "z_codes6", 7: "z_codes7"}
+SCALED = [2,3]
+SUMMED = []
+SCALED_J = len(SCALED) * P
+DIRECT = [6,7]
 UNITS = [(0, 1), (2, 3), (4, 5), (6,), (7,)]
 
 
@@ -50,6 +53,8 @@ def tile_picked_mixup_none_p_kernel(
         xs = keep.tile([P, T], U8, name="xs", align_bytes=64)
         xw = keep.tile([P, T], I32, name="xw", tag="xw", align_bytes=64)
         shares = keep.tile([P, P], F32, name="shares")
+        lam_rows = keep.tile([P, SCALED_J], F32, name="lam_rows")
+        mu_rows = keep.tile([P, SCALED_J], F32, name="mu_rows")
         w2w = keep.tile([P, N], I32, name="w2w", align_bytes=64)
         w2s = keep.tile([P, N], U8, name="w2s", align_bytes=64)
         ident = keep.tile([P, P], F32, name="ident")
@@ -71,13 +76,15 @@ def tile_picked_mixup_none_p_kernel(
             for c in range(0, c1 - c0, P):
                 w_raw.append(raw[:, :, c : c + P].rearrange("p j (q u e) -> p u q e j", u=2, e=2))
         nc.sync.dma_start(pos_sb[:], pos1)
+        nc.sync.dma_start(lam_rows[:], lam[:, SCALED[0] * P : SCALED[0] * P + SCALED_J])
+        nc.sync.dma_start(mu_rows[:], mu[:, SCALED[0] * P : SCALED[0] * P + SCALED_J])
         nc.sync.dma_start(w2w[:], w2_words[0].rearrange("p n t -> p (n t)").bitcast(I32))
         for q in range(4):
             nc.sync.dma_start(w2s[32 * q : 32 * q + 4, :].bitcast(I32), w2_scales[0, 4 * q : 4 * q + 4, :].bitcast(I32))
 
         turned = bank(7)
         nc.tensor.transpose(turned[:, 0:P], shares[:], ident[:])
-        lam_t = keep.tile([P, BLOCKS], F32, name="lam_t", tag="late")
+        lam_t = keep.tile([P, BLOCKS], F32, name="lam_t", tag="late", align_bytes=64)
         mu_t = keep.tile([P, BLOCKS], F32, name="mu_t")
         nc.scalar.copy(lam_t[:], turned[:, 0:BLOCKS])
         nc.scalar.copy(mu_t[:], turned[:, 64 : 64 + BLOCKS])
@@ -144,29 +151,46 @@ def tile_picked_mixup_none_p_kernel(
         def gather(dst, t, j0, n):
             nc.vector.tensor_copy(dst, h[t][:].indirect(entries(pos_sb, j0, n)))
 
-        def gather_half(dst, s, t):
-            cut = HALF // 2 if t == TILES - 1 else HALF
-            for c0 in range(0, HALF, cut):
-                gather(dst[:, c0 : c0 + cut], t, s * HALF + c0, cut)
-
         partner = {}
-        for s, t in [(0, 0), (1, 0), (0, 1), (0, 2), (0, 3)]:
-            g = keep.tile([P, HALF], F32, name="partner%d%d" % (s, t))
-            gather_half(g[:], s, t)
-            partner[(s, t)] = g[:]
 
-        own = []
-        for b in range(BLOCKS):
-            turned = bank(b)
+        def gather_half(s, t, tag, cuts):
+            g = keep.tile([P, HALF], F32, name="partner%d%d" % (s, t), tag=tag, align_bytes=64)
+            for c0, c1 in cuts:
+                gather(g[:, c0:c1], t, s * HALF + c0, c1 - c0)
+            partner[(s, t)] = g
+
+        whole = [(0, HALF)]
+        banks = {}
+        parts_done = []
+
+        def add_part(part, t):
+            parts_done.append(t)
+            for k, b in enumerate(SCALED):
+                turn(banks[b], t, part[:, k * P : (k + 1) * P], start=len(parts_done) == 1, stop=len(parts_done) == 2 * TILES)
+
+        def own_part(t):
+            part = keep.tile([P, SCALED_J], F32, name="own_part%d" % t)
+            nc.gpsimd.tensor_tensor(part[:], h[t][:, SCALED[0] * P : SCALED[0] * P + SCALED_J], lam_rows[:], MULT)
+            add_part(part, t)
+
+        def partner_part(t):
+            part = keep.tile([P, SCALED_J], F32, name="partner_part%d" % t)
+            nc.gpsimd.tensor_tensor(part[:], partner[(0, t)][:, SCALED[0] * P : SCALED[0] * P + SCALED_J], mu_rows[:], MULT)
+            add_part(part, t)
+
+        def turn_own(b, t):
+            turn(banks[b], t, h[t][:, b * P : (b + 1) * P])
+
+        own = {}
+
+        def scale_own(b):
             a = keep.tile([P, H], F32, name="own%d" % b, tag="own%d" % b, align_bytes=64)
-            if b < BLOCKS - 2:
-                for t in range(TILES):
-                    turn(turned, t, h[t][:, b * P : (b + 1) * P])
-                nc.scalar.activation(a[:], turned[:], COPY, scale=lam_t[:, b : b + 1])
+            if b not in DIRECT:
+                nc.scalar.activation(a[:], banks[b][:], COPY, scale=lam_t[:, b : b + 1])
             else:
                 nc.tensor.matmul_mx(
-                    out=turned[:],
-                    lhsT=xg_end[:, b * P - 768 : (b + 1) * P - 768].bitcast(FP8X4),
+                    out=banks[b][:],
+                    lhsT=(xg[:, b * P : (b + 1) * P] if b < 6 else xg_end[:, b * P - 768 : (b + 1) * P - 768]).bitcast(FP8X4),
                     lhsT_scale=xgs[:, b * P : (b + 1) * P],
                     rhs=w_codes[:].bitcast(FP8X4),
                     rhs_scale=w_scales[:],
@@ -175,79 +199,114 @@ def tile_picked_mixup_none_p_kernel(
                 )
                 nc.scalar.activation(
                     a[:].rearrange("p (u t x) -> p u t x", u=2, t=TILES),
-                    turned[:].rearrange("p (t u x) -> p u t x", u=2, t=TILES),
+                    banks[b][:].rearrange("p (t u x) -> p u t x", u=2, t=TILES),
                     COPY,
                     scale=lam_t[:, b : b + 1],
                 )
-            own.append(a)
+            own[b] = a
+            banks[b] = bank(b)
 
-        z_t = []
+        def turn_partner(b, t):
+            turn(banks[b], t, partner[(b // 4, t)][:, (b % 4) * P : (b % 4 + 1) * P])
+
+        z_t = {}
 
         def mix(b):
-            s, c0 = b // 4, (b % 4) * P
-            turned = bank(b)
-            for t in range(TILES):
-                turn(turned, t, partner[(s, t)][:, c0 : c0 + P])
             z = keep.tile([P, H], BF16, name="z%d" % b)
-            nc.vector.scalar_tensor_tensor(z[:], turned[:], mu_t[:, b : b + 1], own[b][:], MULT, ADD)
-            z_t.append(z)
+            if b in SCALED:
+                nc.scalar.copy(z[:], banks[b][:])
+            else:
+                nc.vector.scalar_tensor_tensor(z[:], banks[b][:], mu_t[:, b : b + 1], own[b][:], MULT, ADD)
+            z_t[b] = z
 
         z_grouped = {}
         for unit in UNITS:
-            z_grouped[unit] = keep.tile([P, len(unit) * P, 2], F32, name="z_grouped%d" % unit[0], align_bytes=64)
-
-        def turn_back(unit):
+            grouped = keep.tile([P, len(unit) * P, 2], F32, name="z_grouped%d" % unit[0], align_bytes=64)
             for k, b in enumerate(unit):
-                turned = bank(b)
-                words = z_t[b][:].bitcast(F32)
-                for u in range(2):
-                    nc.tensor.transpose(turned[:, u * P : (u + 1) * P], words[:, u * P : (u + 1) * P], ident[:])
-                nc.scalar.copy(
-                    z_grouped[unit][:, k * P : (k + 1) * P, :], turned[:, 0 : 2 * P].rearrange("p (u j) -> p j u", u=2)
-                )
+                z_grouped[b] = (grouped, k)
 
-        def finish(unit):
+        def turn_back(b):
+            turned = bank(b)
+            words = z_t[b][:].bitcast(F32)
+            for u in range(2):
+                nc.tensor.transpose(turned[:, u * P : (u + 1) * P], words[:, u * P : (u + 1) * P], ident[:])
+            grouped, k = z_grouped[b]
+            nc.scalar.copy(grouped[:, k * P : (k + 1) * P, :], turned[:, 0 : 2 * P].rearrange("p (u j) -> p j u", u=2))
+
+        def finish(unit, codes):
             n = len(unit) * P
             j0 = unit[0] * P
-            grouped = z_grouped[unit]
-            codes = keep.tile([P, n], U32, name="z_codes%d" % unit[0], tag=CODES_TAG[unit[0]], align_bytes=64)
             scales = keep.tile([P, n], U8, name="z_scales%d" % unit[0], align_bytes=64)
             nc.vector.quantize_mx(
-                out=codes[:].bitcast(FP8X4),
+                out=codes.bitcast(FP8X4),
                 scales=scales[:],
-                in_=grouped[:].rearrange("p j u -> p (j u)").bitcast(BF16),
+                in_=z_grouped[unit[0]][0][:].rearrange("p j u -> p (j u)").bitcast(BF16),
             )
             acc = bank(unit[-1])
             nc.tensor.matmul_mx(
                 out=acc[:, 0:n],
                 lhsT=w2w[:].bitcast(FP8X4),
                 lhsT_scale=w2s[:],
-                rhs=codes[:].bitcast(FP8X4),
+                rhs=codes.bitcast(FP8X4),
                 rhs_scale=scales[:],
                 start=True,
                 stop=True,
             )
             res = keep.tile([P, n], F32, name="res%d" % unit[0])
-            nc.scalar.copy(res[:], acc[:, 0:n])
+            if unit[0] in [6,7]:
+                nc.vector.tensor_copy(res[:], acc[:, 0:n])
+            else:
+                nc.scalar.copy(res[:], acc[:, 0:n])
             nc.sync.dma_start(out[:, j0 : j0 + n], res[:])
 
-        mix(0)
-        mix(1)
-        g = keep.tile([P, HALF], F32, name="partner11", tag="own1", align_bytes=64)
-        gather_half(g[:], 1, 1)
-        partner[(1, 1)] = g[:]
-        mix(2)
-        mix(3)
-        late = keep.tile([P, 2, HALF], F32, name="partner_late", tag="late")
-        for t in (2, 3):
-            gather_half(late[:, t - 2, :], 1, t)
-            partner[(1, t)] = late[:, t - 2, :]
-        turn_back(UNITS[0])
-        turn_back(UNITS[1])
-        finish(UNITS[0])
-        for b in range(4, BLOCKS):
+        def sum_back(b, part, first):
+            view = part[:].rearrange("p (u q e) -> p u e q", u=2, e=2)
+            for lane in range(4):
+                nc.tensor.matmul(
+                    banks[b][:, lane * P : (lane + 1) * P], part[:, lane * P : (lane + 1) * P], ident[:],
+                    start=first and lane == 0, stop=(not first) and lane == 3, is_transpose=True,
+                )
+
+        rest = [b for b in range(BLOCKS) if b not in SCALED]
+        for b in range(BLOCKS):
+            banks[b] = bank(b)
+        for t in range(TILES):
+            for s in range(2):
+                gather_half(s, t, "partner%d%d" % (s, t), whole)
+        for t in range(2):
+            for b in rest:
+                if b not in DIRECT:
+                    turn_own(b, t)
+        for b in rest:
+            if b not in DIRECT:
+                turn_own(b, 2)
+                turn_own(b, 3)
+            scale_own(b)
+        for t in range(3):
+            own_part(t)
+            partner_part(t)
+        for b in rest[:2]:
+            for t in range(3):
+                turn_partner(b, t)
+        own_part(3)
+        for t in range(3):
+            turn_partner(4, t)
+        for b in rest[:2]:
+            turn_partner(b, 3)
             mix(b)
-        for unit in UNITS[2:]:
-            turn_back(unit)
-        for unit in UNITS[1:]:
-            finish(unit)
+        partner_part(3)
+        for b in SCALED:
+            mix(b)
+        codes = keep.tile([P, S], U32, name="z_codes", align_bytes=64)
+        for b in range(4, BLOCKS):
+            for t in range(3 if b == 4 else 0, TILES):
+                turn_partner(b, t)
+            mix(b)
+            for e in [[],[],[],[]][b - 4]:
+                turn_back(e)
+            for unit in [[],[],[],[]][b - 4]:
+                finish(unit, codes[:, unit[0] * P : (unit[-1] + 1) * P])
+        for b in range(8):
+            turn_back(b)
+        for unit in UNITS[0:]:
+            finish(unit, codes[:, unit[0] * P : (unit[-1] + 1) * P])

@@ -21,12 +21,15 @@ COPY = mybir.ActivationFunctionType.Copy
 P = 128
 HALF = 512
 BLOCKS = S // P
-TILES = 4
+TILES = H // P
 X_PIECES = [(0, 512), (512, 256), (768, 256)]
-SCALED = [2,3]
-SUMMED = []
-SCALED_J = len(SCALED) * P
-DIRECT = [6,7]
+X_LAST = X_PIECES[2][0]
+W_LOADS = [(0, 128), (128, 256), (256, 512)]
+SCALED = [1, 2, 3]
+SCALED_J0, SCALED_J1 = SCALED[0] * P, (SCALED[-1] + 1) * P
+MIXED = [0, 4, 5, 6, 7]
+DIRECT = [6, 7]
+AHEAD = [4, 5, 6]
 UNITS = [(0, 1), (2, 3), (4, 5), (6,), (7,)]
 
 
@@ -53,8 +56,8 @@ def tile_picked_mixup_none_p_kernel(
         xs = keep.tile([P, T], U8, name="xs", align_bytes=64)
         xw = keep.tile([P, T], I32, name="xw", tag="xw", align_bytes=64)
         shares = keep.tile([P, P], F32, name="shares")
-        lam_rows = keep.tile([P, SCALED_J], F32, name="lam_rows")
-        mu_rows = keep.tile([P, SCALED_J], F32, name="mu_rows")
+        lam_rows = keep.tile([P, SCALED_J1 - SCALED_J0], F32, name="lam_rows")
+        mu_rows = keep.tile([P, SCALED_J1 - SCALED_J0], F32, name="mu_rows")
         w2w = keep.tile([P, N], I32, name="w2w", align_bytes=64)
         w2s = keep.tile([P, N], U8, name="w2s", align_bytes=64)
         ident = keep.tile([P, P], F32, name="ident")
@@ -70,24 +73,24 @@ def tile_picked_mixup_none_p_kernel(
             nc.sync.dma_start(xs[32 * q : 32 * q + 4, :].bitcast(I32), x_scales[0, 4 * q : 4 * q + 4, :].bitcast(I32))
         nc.sync.dma_start(xw[:], x_words[0].rearrange("p n t -> p (n t)").bitcast(I32))
         w_raw = []
-        for c0, c1 in [(0, 128), (128, 256), (256, 512)]:
+        for c0, c1 in W_LOADS:
             raw = keep.tile([P, 4, c1 - c0], F32, name="w_raw%d" % c0)
             nc.sync.dma_start(raw[:], w1[:, c0:c1].rearrange("(p j) c -> p j c", j=4))
             for c in range(0, c1 - c0, P):
                 w_raw.append(raw[:, :, c : c + P].rearrange("p j (q u e) -> p u q e j", u=2, e=2))
         nc.sync.dma_start(pos_sb[:], pos1)
-        nc.sync.dma_start(lam_rows[:], lam[:, SCALED[0] * P : SCALED[0] * P + SCALED_J])
-        nc.sync.dma_start(mu_rows[:], mu[:, SCALED[0] * P : SCALED[0] * P + SCALED_J])
+        nc.sync.dma_start(lam_rows[:], lam[:, SCALED_J0:SCALED_J1])
+        nc.sync.dma_start(mu_rows[:], mu[:, SCALED_J0:SCALED_J1])
         nc.sync.dma_start(w2w[:], w2_words[0].rearrange("p n t -> p (n t)").bitcast(I32))
         for q in range(4):
             nc.sync.dma_start(w2s[32 * q : 32 * q + 4, :].bitcast(I32), w2_scales[0, 4 * q : 4 * q + 4, :].bitcast(I32))
 
-        turned = bank(7)
-        nc.tensor.transpose(turned[:, 0:P], shares[:], ident[:])
-        lam_t = keep.tile([P, BLOCKS], F32, name="lam_t", tag="late", align_bytes=64)
+        shares_turned = bank(BLOCKS - 1)
+        nc.tensor.transpose(shares_turned[:, 0:P], shares[:], ident[:])
+        lam_t = keep.tile([P, BLOCKS], F32, name="lam_t", tag="late")
         mu_t = keep.tile([P, BLOCKS], F32, name="mu_t")
-        nc.scalar.copy(lam_t[:], turned[:, 0:BLOCKS])
-        nc.scalar.copy(mu_t[:], turned[:, 64 : 64 + BLOCKS])
+        nc.scalar.copy(lam_t[:], shares_turned[:, 0:BLOCKS])
+        nc.scalar.copy(mu_t[:], shares_turned[:, 64 : 64 + BLOCKS])
 
         xgs = keep.tile([P, S], U8, name="xgs", align_bytes=64)
         nc.vector.tensor_copy(xgs[:], xs[:].indirect(offs_sb[:]))
@@ -96,9 +99,11 @@ def tile_picked_mixup_none_p_kernel(
         w_scales = keep.tile([P, H], U8, name="w_scales", align_bytes=64)
 
         def quantise_w(t):
-            tag = "xw" if t == TILES - 1 else "w_grouped%d" % t
-            grouped = keep.tile([P, 2, 32, 2, 4], BF16, name="w_grouped%d" % t, tag=tag, align_bytes=64)
-            if t == TILES - 1:
+            last = t == TILES - 1
+            grouped = keep.tile(
+                [P, 2, 32, 2, 4], BF16, name="w_grouped%d" % t, tag="xw" if last else "w_grouped%d" % t, align_bytes=64
+            )
+            if last:
                 nc.vector.tensor_copy(grouped[:], w_raw[t])
             else:
                 nc.scalar.copy(grouped[:], w_raw[t])
@@ -109,17 +114,17 @@ def tile_picked_mixup_none_p_kernel(
             )
 
         quantise_w(0)
-        xg = keep.tile([P, 768], U32, name="xg", align_bytes=64)
-        xg_end = keep.tile([P, 256], U32, name="xg_end", tag="w_grouped0", align_bytes=64)
+        xg = keep.tile([P, X_LAST], U32, name="xg", align_bytes=64)
+        xg_last = keep.tile([P, S - X_LAST], U32, name="xg_last", tag="w_grouped0", align_bytes=64)
 
         def picked(j0, n):
-            return xg[:, j0 : j0 + n] if j0 < 768 else xg_end[:]
+            return xg[:, j0 : j0 + n] if j0 < X_LAST else xg_last[:, j0 - X_LAST : j0 - X_LAST + n]
 
         for j0, n in X_PIECES:
             nc.vector.tensor_copy(picked(j0, n), xw[:].bitcast(U32).indirect(entries(offs_sb, j0, n)))
         quantise_w(1)
 
-        def first_product(t, b, pieces, on_vector):
+        def first_product(t, b, pieces, copy):
             acc = bank(b)
             j_first = pieces[0][0]
             for j0, n in pieces:
@@ -133,64 +138,36 @@ def tile_picked_mixup_none_p_kernel(
                     stop=True,
                 )
             width = sum(n for j0, n in pieces)
-            if on_vector:
-                nc.vector.tensor_copy(h[t][:, j_first : j_first + width], acc[:, 0:width])
-            else:
-                nc.scalar.copy(h[t][:, j_first : j_first + width], acc[:, 0:width])
+            copy(h[t][:, j_first : j_first + width], acc[:, 0:width])
 
         h = [keep.tile([P, S], F32, name="h%d" % t) for t in range(TILES)]
-        first_product(0, 0, X_PIECES[0:1], False)
-        first_product(0, 1, X_PIECES[1:2], False)
-        first_product(0, 7, X_PIECES[2:3], False)
+        first_product(0, 0, X_PIECES[0:1], nc.vector.tensor_copy)
+        first_product(0, 1, X_PIECES[1:2], nc.scalar.copy)
+        first_product(0, BLOCKS - 1, X_PIECES[2:3], nc.scalar.copy)
         for t in range(1, TILES):
             if t + 1 < TILES:
                 quantise_w(t + 1)
-            first_product(t, 2 * t, X_PIECES[0:1], False)
-            first_product(t, 2 * t + 1, X_PIECES[1:3], False)
+            first_product(t, 2 * t, X_PIECES[0:1], nc.scalar.copy)
+            first_product(t, 2 * t + 1, X_PIECES[1:3], nc.scalar.copy)
 
-        def gather(dst, t, j0, n):
-            nc.vector.tensor_copy(dst, h[t][:].indirect(entries(pos_sb, j0, n)))
-
+        banks = [bank(b) for b in range(BLOCKS)]
         partner = {}
+        own = {}
+        z_turned = {}
 
-        def gather_half(s, t, tag, cuts):
-            g = keep.tile([P, HALF], F32, name="partner%d%d" % (s, t), tag=tag, align_bytes=64)
-            for c0, c1 in cuts:
-                gather(g[:, c0:c1], t, s * HALF + c0, c1 - c0)
-            partner[(s, t)] = g
-
-        whole = [(0, HALF)]
-        banks = {}
-        parts_done = []
-
-        def add_part(part, t):
-            parts_done.append(t)
-            for k, b in enumerate(SCALED):
-                turn(banks[b], t, part[:, k * P : (k + 1) * P], start=len(parts_done) == 1, stop=len(parts_done) == 2 * TILES)
-
-        def own_part(t):
-            part = keep.tile([P, SCALED_J], F32, name="own_part%d" % t)
-            nc.gpsimd.tensor_tensor(part[:], h[t][:, SCALED[0] * P : SCALED[0] * P + SCALED_J], lam_rows[:], MULT)
-            add_part(part, t)
-
-        def partner_part(t):
-            part = keep.tile([P, SCALED_J], F32, name="partner_part%d" % t)
-            nc.gpsimd.tensor_tensor(part[:], partner[(0, t)][:, SCALED[0] * P : SCALED[0] * P + SCALED_J], mu_rows[:], MULT)
-            add_part(part, t)
+        def gather_partner(s, t, dst):
+            nc.vector.tensor_copy(dst, h[t][:].indirect(entries(pos_sb, s * HALF, HALF)))
+            partner[(s, t)] = dst
 
         def turn_own(b, t):
             turn(banks[b], t, h[t][:, b * P : (b + 1) * P])
 
-        own = {}
-
         def scale_own(b):
-            a = keep.tile([P, H], F32, name="own%d" % b, tag="own%d" % b, align_bytes=64)
-            if b not in DIRECT:
-                nc.scalar.activation(a[:], banks[b][:], COPY, scale=lam_t[:, b : b + 1])
-            else:
+            scaled = keep.tile([P, H], F32, name="own%d" % b)
+            if b in DIRECT:
                 nc.tensor.matmul_mx(
                     out=banks[b][:],
-                    lhsT=(xg[:, b * P : (b + 1) * P] if b < 6 else xg_end[:, b * P - 768 : (b + 1) * P - 768]).bitcast(FP8X4),
+                    lhsT=picked(b * P, P).bitcast(FP8X4),
                     lhsT_scale=xgs[:, b * P : (b + 1) * P],
                     rhs=w_codes[:].bitcast(FP8X4),
                     rhs_scale=w_scales[:],
@@ -198,18 +175,31 @@ def tile_picked_mixup_none_p_kernel(
                     stop=True,
                 )
                 nc.scalar.activation(
-                    a[:].rearrange("p (u t x) -> p u t x", u=2, t=TILES),
+                    scaled[:].rearrange("p (u t x) -> p u t x", u=2, t=TILES),
                     banks[b][:].rearrange("p (t u x) -> p u t x", u=2, t=TILES),
                     COPY,
                     scale=lam_t[:, b : b + 1],
                 )
-            own[b] = a
+            else:
+                nc.scalar.activation(scaled[:], banks[b][:], COPY, scale=lam_t[:, b : b + 1])
+            own[b] = scaled
             banks[b] = bank(b)
 
-        def turn_partner(b, t):
-            turn(banks[b], t, partner[(b // 4, t)][:, (b % 4) * P : (b % 4 + 1) * P])
+        def add_product(name, t, values, factor, start, stop):
+            product = keep.tile([P, SCALED_J1 - SCALED_J0], F32, name="%s%d" % (name, t))
+            nc.gpsimd.tensor_tensor(product[:], values[:, SCALED_J0:SCALED_J1], factor[:], MULT)
+            for k, b in enumerate(SCALED):
+                turn(banks[b], t, product[:, k * P : (k + 1) * P], start=start, stop=stop)
 
-        z_t = {}
+        def add_own(t):
+            add_product("own_product", t, h[t], lam_rows, t == 0, False)
+
+        def add_partner(t):
+            add_product("partner_product", t, partner[(0, t)], mu_rows, False, t == TILES - 1)
+
+        def turn_partner(b, t):
+            s, c0 = divmod(b * P, HALF)
+            turn(banks[b], t, partner[(s, t)][:, c0 : c0 + P])
 
         def mix(b):
             z = keep.tile([P, H], BF16, name="z%d" % b)
@@ -217,96 +207,79 @@ def tile_picked_mixup_none_p_kernel(
                 nc.scalar.copy(z[:], banks[b][:])
             else:
                 nc.vector.scalar_tensor_tensor(z[:], banks[b][:], mu_t[:, b : b + 1], own[b][:], MULT, ADD)
-            z_t[b] = z
+            z_turned[b] = z
 
-        z_grouped = {}
+        for t in range(TILES):
+            for s in range(2 if t < 2 else 1):
+                dst = keep.tile([P, HALF], F32, name="partner%d%d" % (s, t))
+                gather_partner(s, t, dst[:])
+        for t in range(2):
+            for b in MIXED:
+                if b not in DIRECT:
+                    turn_own(b, t)
+        for b in MIXED:
+            if b not in DIRECT:
+                turn_own(b, 2)
+                turn_own(b, 3)
+            scale_own(b)
+        late = keep.tile([P, 2, HALF], F32, name="partner_late", tag="late")
+        for t in (2, 3):
+            gather_partner(1, t, late[:, t - 2, :])
+
+        for t in range(2):
+            add_own(t)
+            add_partner(t)
+        for t in range(3):
+            turn_partner(0, t)
+        add_own(2)
+        add_partner(2)
+        for t in range(2):
+            for b in AHEAD:
+                turn_partner(b, t)
+        add_own(3)
+        turn_partner(0, 3)
+        mix(0)
+        add_partner(3)
+        for b in SCALED:
+            mix(b)
+        for b in MIXED[1:]:
+            for t in range(2 if b in AHEAD else 0, TILES):
+                turn_partner(b, t)
+            mix(b)
+
+        z_grouped = []
         for unit in UNITS:
             grouped = keep.tile([P, len(unit) * P, 2], F32, name="z_grouped%d" % unit[0], align_bytes=64)
             for k, b in enumerate(unit):
-                z_grouped[b] = (grouped, k)
+                back = bank(b)
+                words = z_turned[b][:].bitcast(F32)
+                for u in range(2):
+                    nc.tensor.transpose(back[:, u * P : (u + 1) * P], words[:, u * P : (u + 1) * P], ident[:])
+                nc.scalar.copy(grouped[:, k * P : (k + 1) * P, :], back[:, 0 : 2 * P].rearrange("p (u j) -> p j u", u=2))
+            z_grouped.append(grouped)
 
-        def turn_back(b):
-            turned = bank(b)
-            words = z_t[b][:].bitcast(F32)
-            for u in range(2):
-                nc.tensor.transpose(turned[:, u * P : (u + 1) * P], words[:, u * P : (u + 1) * P], ident[:])
-            grouped, k = z_grouped[b]
-            nc.scalar.copy(grouped[:, k * P : (k + 1) * P, :], turned[:, 0 : 2 * P].rearrange("p (u j) -> p j u", u=2))
-
-        def finish(unit, codes):
-            n = len(unit) * P
-            j0 = unit[0] * P
-            scales = keep.tile([P, n], U8, name="z_scales%d" % unit[0], align_bytes=64)
+        z_codes = keep.tile([P, S], U32, name="z_codes", align_bytes=64)
+        for unit, grouped in zip(UNITS, z_grouped):
+            j0, n = unit[0] * P, len(unit) * P
+            z_scales = keep.tile([P, n], U8, name="z_scales%d" % unit[0], align_bytes=64)
             nc.vector.quantize_mx(
-                out=codes.bitcast(FP8X4),
-                scales=scales[:],
-                in_=z_grouped[unit[0]][0][:].rearrange("p j u -> p (j u)").bitcast(BF16),
+                out=z_codes[:, j0 : j0 + n].bitcast(FP8X4),
+                scales=z_scales[:],
+                in_=grouped[:].rearrange("p j u -> p (j u)").bitcast(BF16),
             )
             acc = bank(unit[-1])
             nc.tensor.matmul_mx(
                 out=acc[:, 0:n],
                 lhsT=w2w[:].bitcast(FP8X4),
                 lhsT_scale=w2s[:],
-                rhs=codes.bitcast(FP8X4),
-                rhs_scale=scales[:],
+                rhs=z_codes[:, j0 : j0 + n].bitcast(FP8X4),
+                rhs_scale=z_scales[:],
                 start=True,
                 stop=True,
             )
             res = keep.tile([P, n], F32, name="res%d" % unit[0])
-            if unit[0] in [6,7]:
+            if len(unit) == 1:
                 nc.vector.tensor_copy(res[:], acc[:, 0:n])
             else:
                 nc.scalar.copy(res[:], acc[:, 0:n])
             nc.sync.dma_start(out[:, j0 : j0 + n], res[:])
-
-        def sum_back(b, part, first):
-            view = part[:].rearrange("p (u q e) -> p u e q", u=2, e=2)
-            for lane in range(4):
-                nc.tensor.matmul(
-                    banks[b][:, lane * P : (lane + 1) * P], part[:, lane * P : (lane + 1) * P], ident[:],
-                    start=first and lane == 0, stop=(not first) and lane == 3, is_transpose=True,
-                )
-
-        rest = [b for b in range(BLOCKS) if b not in SCALED]
-        for b in range(BLOCKS):
-            banks[b] = bank(b)
-        for t in range(TILES):
-            for s in range(2):
-                gather_half(s, t, "partner%d%d" % (s, t), whole)
-        for t in range(2):
-            for b in rest:
-                if b not in DIRECT:
-                    turn_own(b, t)
-        for b in rest:
-            if b not in DIRECT:
-                turn_own(b, 2)
-                turn_own(b, 3)
-            scale_own(b)
-        for t in range(3):
-            own_part(t)
-            partner_part(t)
-        for b in rest[:2]:
-            for t in range(3):
-                turn_partner(b, t)
-        own_part(3)
-        for t in range(3):
-            turn_partner(4, t)
-        for b in rest[:2]:
-            turn_partner(b, 3)
-            mix(b)
-        partner_part(3)
-        for b in SCALED:
-            mix(b)
-        codes = keep.tile([P, S], U32, name="z_codes", align_bytes=64)
-        for b in range(4, BLOCKS):
-            for t in range(3 if b == 4 else 0, TILES):
-                turn_partner(b, t)
-            mix(b)
-            for e in [[],[],[],[]][b - 4]:
-                turn_back(e)
-            for unit in [[],[],[],[]][b - 4]:
-                finish(unit, codes[:, unit[0] * P : (unit[-1] + 1) * P])
-        for b in range(8):
-            turn_back(b)
-        for unit in UNITS[0:]:
-            finish(unit, codes[:, unit[0] * P : (unit[-1] + 1) * P])

@@ -29,7 +29,6 @@ SCALED = [1, 2, 3]
 SCALED_J0, SCALED_J1 = SCALED[0] * P, (SCALED[-1] + 1) * P
 MIXED = [0, 4, 5, 6, 7]
 DIRECT = [6, 7]
-AHEAD = [4, 5, 6]
 UNITS = [(0, 1), (2, 3), (4, 5), (6,), (7,)]
 
 
@@ -87,8 +86,10 @@ def tile_picked_mixup_none_p_kernel(
 
         shares_turned = bank(BLOCKS - 1)
         nc.tensor.transpose(shares_turned[:, 0:P], shares[:], ident[:])
-        lam_t = keep.tile([P, BLOCKS], F32, name="lam_t", tag="late")
+        lam_t = keep.tile([P, BLOCKS], F32, name="lam_t")
+        lam_first = keep.tile([P, 1], F32, name="lam_first", tag="late")
         mu_t = keep.tile([P, BLOCKS], F32, name="mu_t")
+        nc.scalar.copy(lam_first[:], shares_turned[:, 0:1])
         nc.scalar.copy(lam_t[:], shares_turned[:, 0:BLOCKS])
         nc.scalar.copy(mu_t[:], shares_turned[:, 64 : 64 + BLOCKS])
 
@@ -141,8 +142,8 @@ def tile_picked_mixup_none_p_kernel(
             copy(h[t][:, j_first : j_first + width], acc[:, 0:width])
 
         h = [keep.tile([P, S], F32, name="h%d" % t) for t in range(TILES)]
-        first_product(0, 0, X_PIECES[0:1], nc.vector.tensor_copy)
-        first_product(0, 1, X_PIECES[1:2], nc.scalar.copy)
+        first_product(0, 0, X_PIECES[0:1], nc.scalar.copy)
+        first_product(0, 1, X_PIECES[1:2], nc.vector.tensor_copy)
         first_product(0, BLOCKS - 1, X_PIECES[2:3], nc.scalar.copy)
         for t in range(1, TILES):
             if t + 1 < TILES:
@@ -181,7 +182,8 @@ def tile_picked_mixup_none_p_kernel(
                     scale=lam_t[:, b : b + 1],
                 )
             else:
-                nc.scalar.activation(scaled[:], banks[b][:], COPY, scale=lam_t[:, b : b + 1])
+                scale = lam_first[:] if b == 0 else lam_t[:, b : b + 1]
+                nc.scalar.activation(scaled[:], banks[b][:], COPY, scale=scale)
             own[b] = scaled
             banks[b] = bank(b)
 
@@ -210,7 +212,7 @@ def tile_picked_mixup_none_p_kernel(
             z_turned[b] = z
 
         for t in range(TILES):
-            for s in range(2 if t < 2 else 1):
+            for s in range(2 if t == 0 else 1):
                 dst = keep.tile([P, HALF], F32, name="partner%d%d" % (s, t))
                 gather_partner(s, t, dst[:])
         for t in range(2):
@@ -222,9 +224,9 @@ def tile_picked_mixup_none_p_kernel(
                 turn_own(b, 2)
                 turn_own(b, 3)
             scale_own(b)
-        late = keep.tile([P, 2, HALF], F32, name="partner_late", tag="late")
-        for t in (2, 3):
-            gather_partner(1, t, late[:, t - 2, :])
+        late = keep.tile([P, TILES - 1, HALF], F32, name="partner_late", tag="late")
+        for t in range(1, TILES):
+            gather_partner(1, t, late[:, t - 1, :])
 
         for t in range(2):
             add_own(t)
@@ -234,7 +236,7 @@ def tile_picked_mixup_none_p_kernel(
         add_own(2)
         add_partner(2)
         for t in range(2):
-            for b in AHEAD:
+            for b in MIXED[1:]:
                 turn_partner(b, t)
         add_own(3)
         turn_partner(0, 3)
@@ -243,7 +245,7 @@ def tile_picked_mixup_none_p_kernel(
         for b in SCALED:
             mix(b)
         for b in MIXED[1:]:
-            for t in range(2 if b in AHEAD else 0, TILES):
+            for t in range(2, TILES):
                 turn_partner(b, t)
             mix(b)
 

@@ -63,7 +63,8 @@ def tile_picked_mixup_none_p_kernel(
 
         nc.vector.memset(xs[:].bitcast(I32), 0)
         nc.vector.memset(w2s[:].bitcast(I32), 0)
-        make_identity(nc, ident[:])
+        nc.vector.memset(ident[:], 0.0)
+        make_identity(nc, ident[:], nomemset=True)
 
         nc.sync.dma_start(offs_sb[:], offs)
         nc.sync.dma_start(shares[0:64, :], lam[0:8, :].rearrange("r (b c) -> (r b) c", c=P))
@@ -188,7 +189,9 @@ def tile_picked_mixup_none_p_kernel(
             banks[b] = bank(b)
 
         def add_product(name, t, values, factor, start, stop):
-            product = keep.tile([P, SCALED_J1 - SCALED_J0], F32, name="%s%d" % (name, t))
+            product = keep.tile(
+                [P, SCALED_J1 - SCALED_J0], F32, name="%s%d" % (name, t), tag="xw" if start else "%s%d" % (name, t), align_bytes=64
+            )
             nc.gpsimd.tensor_tensor(product[:], values[:, SCALED_J0:SCALED_J1], factor[:], MULT)
             for k, b in enumerate(SCALED):
                 turn(banks[b], t, product[:, k * P : (k + 1) * P], start=start, stop=stop)
@@ -225,8 +228,11 @@ def tile_picked_mixup_none_p_kernel(
                 turn_own(b, 3)
             scale_own(b)
         late = keep.tile([P, TILES - 1, HALF], F32, name="partner_late", tag="late")
-        for t in range(1, TILES):
+        for t in range(1, TILES - 1):
             gather_partner(1, t, late[:, t - 1, :])
+        for j0 in (0, 256):
+            nc.vector.tensor_copy(late[:, 2, j0 : j0 + 256], h[3][:].indirect(entries(pos_sb, HALF + j0, 256)))
+        partner[(1, 3)] = late[:, 2, :]
 
         for t in range(2):
             add_own(t)
@@ -280,7 +286,7 @@ def tile_picked_mixup_none_p_kernel(
                 stop=True,
             )
             res = keep.tile([P, n], F32, name="res%d" % unit[0])
-            if len(unit) == 1:
+            if unit == UNITS[-1]:
                 nc.vector.tensor_copy(res[:], acc[:, 0:n])
             else:
                 nc.scalar.copy(res[:], acc[:, 0:n])

@@ -61,14 +61,15 @@ def tile_picked_mixup_none_p_kernel(
         w2s = keep.tile([P, N], U8, name="w2s", align_bytes=64)
         ident = keep.tile([P, P], F32, name="ident")
 
+        nc.vector.memset(shares[:], 0.0)
         nc.vector.memset(xs[:].bitcast(I32), 0)
         nc.vector.memset(w2s[:].bitcast(I32), 0)
         nc.vector.memset(ident[:], 0.0)
         make_identity(nc, ident[:], nomemset=True)
 
         nc.sync.dma_start(offs_sb[:], offs)
-        nc.sync.dma_start(shares[0:64, :], lam[0:8, :].rearrange("r (b c) -> (r b) c", c=P))
-        nc.sync.dma_start(shares[64:128, :], mu[0:8, :].rearrange("r (b c) -> (r b) c", c=P))
+        nc.sync.dma_start(shares[0:BLOCKS, :], lam[0, :].rearrange("(b c) -> b c", c=P))
+        nc.sync.dma_start(shares[BLOCKS : 2 * BLOCKS, :], mu[0, :].rearrange("(b c) -> b c", c=P))
         for q in range(4):
             nc.sync.dma_start(xs[32 * q : 32 * q + 4, :].bitcast(I32), x_scales[0, 4 * q : 4 * q + 4, :].bitcast(I32))
         nc.sync.dma_start(xw[:], x_words[0].rearrange("p n t -> p (n t)").bitcast(I32))
@@ -92,7 +93,7 @@ def tile_picked_mixup_none_p_kernel(
         mu_t = keep.tile([P, BLOCKS], F32, name="mu_t")
         nc.scalar.copy(lam_first[:], shares_turned[:, 0:1])
         nc.scalar.copy(lam_t[:], shares_turned[:, 0:BLOCKS])
-        nc.scalar.copy(mu_t[:], shares_turned[:, 64 : 64 + BLOCKS])
+        nc.scalar.copy(mu_t[:], shares_turned[:, BLOCKS : 2 * BLOCKS])
 
         xgs = keep.tile([P, S], U8, name="xgs", align_bytes=64)
         nc.vector.tensor_copy(xgs[:], xs[:].indirect(offs_sb[:]))

@@ -61,7 +61,7 @@ def tile_picked_mixup_none_p_kernel(
         w2s = keep.tile([P, N], U8, name="w2s", align_bytes=64)
         ident = keep.tile([P, P], F32, name="ident")
 
-        nc.vector.memset(shares[:], 0.0)
+        nc.gpsimd.memset(shares[:], 0.0)
         nc.vector.memset(xs[:].bitcast(I32), 0)
         nc.vector.memset(w2s[:].bitcast(I32), 0)
         nc.vector.memset(ident[:], 0.0)

@@ -78,7 +78,7 @@ def tile_picked_mixup_none_p_kernel(
             raw = keep.tile([P, 4, c1 - c0], F32, name="w_raw%d" % c0)
             nc.sync.dma_start(raw[:], w1[:, c0:c1].rearrange("(p j) c -> p j c", j=4))
             for c in range(0, c1 - c0, P):
-                w_raw.append(raw[:, :, c : c + P].rearrange("p j (q u e) -> p u q e j", u=2, e=2))
+                w_raw.append(raw[:, :, c : c + P].rearrange("p j (q u e) -> p q j u e", u=2, e=2))
         nc.sync.dma_start(pos_sb[:], pos1)
         nc.sync.dma_start(lam_rows[:], lam[:, SCALED_J0:SCALED_J1])
         nc.sync.dma_start(mu_rows[:], mu[:, SCALED_J0:SCALED_J1])
@@ -107,9 +107,9 @@ def tile_picked_mixup_none_p_kernel(
                 [P, 2, 32, 2, 4], BF16, name="w_grouped%d" % t, tag="xw" if last else "w_grouped%d" % t, align_bytes=64
             )
             if last:
-                nc.vector.tensor_copy(grouped[:], w_raw[t])
+                nc.vector.tensor_copy(grouped[:].rearrange("p u q e j -> p q j u e"), w_raw[t])
             else:
-                nc.scalar.copy(grouped[:], w_raw[t])
+                nc.scalar.copy(grouped[:].rearrange("p u q e j -> p q j u e"), w_raw[t])
             nc.vector.quantize_mx(
                 out=w_codes[:, t * P : (t + 1) * P].bitcast(FP8X4),
                 scales=w_scales[:, t * P : (t + 1) * P],

@@ -25,9 +25,9 @@ TILES = H // P
 X_PIECES = [(0, 512), (512, 256), (768, 256)]
 X_LAST = X_PIECES[2][0]
 W_LOADS = [(0, 128), (128, 256), (256, 512)]
-SCALED = [1, 2, 3]
+SCALED = [2, 3]
 SCALED_J0, SCALED_J1 = SCALED[0] * P, (SCALED[-1] + 1) * P
-MIXED = [0, 4, 5, 6, 7]
+MIXED = [0, 1, 4, 5, 6, 7]
 DIRECT = [6, 7]
 UNITS = [(0, 1), (2, 3), (4, 5), (6,), (7,)]
 
@@ -229,8 +229,9 @@ def tile_picked_mixup_none_p_kernel(
                 turn_own(b, 3)
             scale_own(b)
         late = keep.tile([P, TILES - 1, HALF], F32, name="partner_late", tag="late")
-        for t in range(1, TILES - 1):
-            gather_partner(1, t, late[:, t - 1, :])
+        gather_partner(1, 1, late[:, 0, :])
+        nc.scalar.activation(late[:, 1, :], h[2][:].indirect(entries(pos_sb, HALF, HALF)), COPY)
+        partner[(1, 2)] = late[:, 1, :]
         for j0 in (0, 256):
             nc.vector.tensor_copy(late[:, 2, j0 : j0 + 256], h[3][:].indirect(entries(pos_sb, HALF + j0, 256)))
         partner[(1, 3)] = late[:, 2, :]
@@ -238,20 +239,22 @@ def tile_picked_mixup_none_p_kernel(
         for t in range(2):
             add_own(t)
             add_partner(t)
-        for t in range(3):
-            turn_partner(0, t)
+        for b in MIXED[:2]:
+            for t in range(3):
+                turn_partner(b, t)
         add_own(2)
         add_partner(2)
         for t in range(2):
-            for b in MIXED[1:]:
+            for b in MIXED[2:]:
                 turn_partner(b, t)
         add_own(3)
-        turn_partner(0, 3)
-        mix(0)
+        for b in MIXED[:2]:
+            turn_partner(b, 3)
+            mix(b)
         add_partner(3)
         for b in SCALED:
             mix(b)
-        for b in MIXED[1:]:
+        for b in MIXED[2:]:
             for t in range(2, TILES):
                 turn_partner(b, t)
             mix(b)

@@ -61,17 +61,17 @@ def tile_picked_mixup_none_p_kernel(
         w2s = keep.tile([P, N], U8, name="w2s", align_bytes=64)
         ident = keep.tile([P, P], F32, name="ident")
 
-        nc.gpsimd.memset(shares[:], 0.0)
-        nc.vector.memset(xs[:].bitcast(I32), 0)
+        nc.gpsimd.memset(xs[:].bitcast(I32), 0)
+        nc.vector.memset(shares[:], 0.0)
         nc.vector.memset(w2s[:].bitcast(I32), 0)
         nc.vector.memset(ident[:], 0.0)
         make_identity(nc, ident[:], nomemset=True)
 
         nc.sync.dma_start(offs_sb[:], offs)
-        nc.sync.dma_start(shares[0:BLOCKS, :], lam[0, :].rearrange("(b c) -> b c", c=P))
-        nc.sync.dma_start(shares[BLOCKS : 2 * BLOCKS, :], mu[0, :].rearrange("(b c) -> b c", c=P))
         for q in range(4):
             nc.sync.dma_start(xs[32 * q : 32 * q + 4, :].bitcast(I32), x_scales[0, 4 * q : 4 * q + 4, :].bitcast(I32))
+        nc.sync.dma_start(shares[0:BLOCKS, :], lam[0, :].rearrange("(b c) -> b c", c=P))
+        nc.sync.dma_start(shares[BLOCKS : 2 * BLOCKS, :], mu[0, :].rearrange("(b c) -> b c", c=P))
         nc.sync.dma_start(xw[:], x_words[0].rearrange("p n t -> p (n t)").bitcast(I32))
         w_raw = []
         for c0, c1 in W_LOADS:
@@ -216,9 +216,8 @@ def tile_picked_mixup_none_p_kernel(
             z_turned[b] = z
 
         for t in range(TILES):
-            for s in range(2 if t == 0 else 1):
-                dst = keep.tile([P, HALF], F32, name="partner%d%d" % (s, t))
-                gather_partner(s, t, dst[:])
+            dst = keep.tile([P, HALF], F32, name="partner0%d" % t)
+            gather_partner(0, t, dst[:])
         for t in range(2):
             for b in MIXED:
                 if b not in DIRECT:
@@ -228,13 +227,12 @@ def tile_picked_mixup_none_p_kernel(
                 turn_own(b, 2)
                 turn_own(b, 3)
             scale_own(b)
-        late = keep.tile([P, TILES - 1, HALF], F32, name="partner_late", tag="late")
-        gather_partner(1, 1, late[:, 0, :])
-        nc.scalar.activation(late[:, 1, :], h[2][:].indirect(entries(pos_sb, HALF, HALF)), COPY)
-        partner[(1, 2)] = late[:, 1, :]
-        for j0 in (0, 256):
-            nc.vector.tensor_copy(late[:, 2, j0 : j0 + 256], h[3][:].indirect(entries(pos_sb, HALF + j0, 256)))
-        partner[(1, 3)] = late[:, 2, :]
+        late = keep.tile([P, TILES, HALF], F32, name="partner_late", tag="late")
+        gather_partner(1, 0, late[:, 0, :])
+        for t in range(1, TILES):
+            nc.vector.tensor_copy(late[:, t, 0:256], h[t][:].indirect(entries(pos_sb, HALF, 256)))
+            nc.scalar.activation(late[:, t, 256:512], h[t][:].indirect(entries(pos_sb, HALF + 256, 256)), COPY)
+            partner[(1, t)] = late[:, t, :]
 
         for t in range(2):
             add_own(t)
@@ -244,9 +242,8 @@ def tile_picked_mixup_none_p_kernel(
                 turn_partner(b, t)
         add_own(2)
         add_partner(2)
-        for t in range(2):
-            for b in MIXED[2:]:
-                turn_partner(b, t)
+        for b in MIXED[2:]:
+            turn_partner(b, 0)
         add_own(3)
         for b in MIXED[:2]:
             turn_partner(b, 3)
@@ -255,7 +252,7 @@ def tile_picked_mixup_none_p_kernel(
         for b in SCALED:
             mix(b)
         for b in MIXED[2:]:
-            for t in range(2, TILES):
+            for t in range(1, TILES):
                 turn_partner(b, t)
             mix(b)
 
@@ -290,7 +287,7 @@ def tile_picked_mixup_none_p_kernel(
                 stop=True,
             )
             res = keep.tile([P, n], F32, name="res%d" % unit[0])
-            if unit == UNITS[-1]:
+            if len(unit) == 1:
                 nc.vector.tensor_copy(res[:], acc[:, 0:n])
             else:
                 nc.scalar.copy(res[:], acc[:, 0:n])

@@ -61,17 +61,17 @@ def tile_picked_mixup_none_p_kernel(
         w2s = keep.tile([P, N], U8, name="w2s", align_bytes=64)
         ident = keep.tile([P, P], F32, name="ident")
 
-        nc.gpsimd.memset(xs[:].bitcast(I32), 0)
-        nc.vector.memset(shares[:], 0.0)
+        nc.gpsimd.memset(shares[:], 0.0)
+        nc.vector.memset(xs[:].bitcast(I32), 0)
         nc.vector.memset(w2s[:].bitcast(I32), 0)
         nc.vector.memset(ident[:], 0.0)
         make_identity(nc, ident[:], nomemset=True)
 
         nc.sync.dma_start(offs_sb[:], offs)
-        for q in range(4):
-            nc.sync.dma_start(xs[32 * q : 32 * q + 4, :].bitcast(I32), x_scales[0, 4 * q : 4 * q + 4, :].bitcast(I32))
         nc.sync.dma_start(shares[0:BLOCKS, :], lam[0, :].rearrange("(b c) -> b c", c=P))
         nc.sync.dma_start(shares[BLOCKS : 2 * BLOCKS, :], mu[0, :].rearrange("(b c) -> b c", c=P))
+        for q in range(4):
+            nc.sync.dma_start(xs[32 * q : 32 * q + 4, :].bitcast(I32), x_scales[0, 4 * q : 4 * q + 4, :].bitcast(I32))
         nc.sync.dma_start(xw[:], x_words[0].rearrange("p n t -> p (n t)").bitcast(I32))
         w_raw = []
         for c0, c1 in W_LOADS:

@@ -16,20 +16,19 @@ U8 = mybir.dt.uint8
 FP8X4 = mybir.dt.float8_e4m3fn_x4
 MULT = mybir.AluOpType.mult
 ADD = mybir.AluOpType.add
+SUB = mybir.AluOpType.subtract
+IS_GE = mybir.AluOpType.is_ge
 COPY = mybir.ActivationFunctionType.Copy
+ABS = mybir.ActivationFunctionType.Abs
 
 P = 128
 HALF = 512
 BLOCKS = S // P
 TILES = H // P
-X_PIECES = [(0, 512), (512, 256), (768, 256)]
-X_LAST = X_PIECES[2][0]
+X_PIECES = [(0, 512), (512, 512)]
 W_LOADS = [(0, 128), (128, 256), (256, 512)]
-SCALED = [2, 3]
-SCALED_J0, SCALED_J1 = SCALED[0] * P, (SCALED[-1] + 1) * P
-MIXED = [0, 1, 4, 5, 6, 7]
-DIRECT = [6, 7]
 UNITS = [(0, 1), (2, 3), (4, 5), (6,), (7,)]
+PAIR = 2 * P
 
 
 def tile_picked_mixup_none_p_kernel(
@@ -38,28 +37,32 @@ def tile_picked_mixup_none_p_kernel(
     nc = tc.nc
     with ExitStack() as ctx:
         keep = ctx.enter_context(tc.tile_pool(name="keep", bufs=1))
+        reuse = ctx.enter_context(tc.tile_pool(name="reuse", bufs=1))
         psum = ctx.enter_context(tc.psum_pool(name="psum", bufs=1))
 
         def bank(b):
             return psum.tile([P, HALF], F32, name="bank%d" % b, tag="bank%d" % b)
 
+        def tile(name, shape, dtype, tag=None):
+            return keep.tile(shape, dtype, name=name, tag=tag or name, align_bytes=64)
+
+        def over_words(name, shape, dtype, offset):
+            return reuse.tile(shape, dtype, name=name, offset=offset, align_bytes=64)
+
         def entries(lst, j0, n):
             return lst[:, j0 // 16 : (j0 + n) // 16]
 
-        def turn(dst_bank, t, src, start=True, stop=True):
-            dst = dst_bank[:].rearrange("p (u t x) -> p u t x", u=2, t=TILES)[:, :, t, :]
-            nc.tensor.matmul(dst, src, ident[:], start=start, stop=stop, is_transpose=True)
+        def turn(dst_bank, t, src, start, stop):
+            nc.tensor.matmul(dst_bank[:, t * P : (t + 1) * P], src, ident[:], start=start, stop=stop, is_transpose=True)
 
         offs_sb = keep.tile([P, S // 16], U16, name="offs_sb")
         pos_sb = keep.tile([P, S // 16], U16, name="pos_sb")
-        xs = keep.tile([P, T], U8, name="xs", align_bytes=64)
-        xw = keep.tile([P, T], I32, name="xw", tag="xw", align_bytes=64)
-        shares = keep.tile([P, P], F32, name="shares")
-        lam_rows = keep.tile([P, SCALED_J1 - SCALED_J0], F32, name="lam_rows")
-        mu_rows = keep.tile([P, SCALED_J1 - SCALED_J0], F32, name="mu_rows")
-        w2w = keep.tile([P, N], I32, name="w2w", align_bytes=64)
-        w2s = keep.tile([P, N], U8, name="w2s", align_bytes=64)
-        ident = keep.tile([P, P], F32, name="ident")
+        xs = tile("xs", [P, T], U8)
+        xw = over_words("xw", [P, T], I32, 0)
+        shares = tile("shares", [P, P], F32)
+        w2w = tile("w2w", [P, N], I32)
+        w2s = tile("w2s", [P, N], U8)
+        ident = tile("ident", [P, P], F32)
 
         nc.gpsimd.memset(shares[:], 0.0)
         nc.vector.memset(xs[:].bitcast(I32), 0)
@@ -68,64 +71,101 @@ def tile_picked_mixup_none_p_kernel(
         make_identity(nc, ident[:], nomemset=True)
 
         nc.sync.dma_start(offs_sb[:], offs)
-        nc.sync.dma_start(shares[0:BLOCKS, :], lam[0, :].rearrange("(b c) -> b c", c=P))
-        nc.sync.dma_start(shares[BLOCKS : 2 * BLOCKS, :], mu[0, :].rearrange("(b c) -> b c", c=P))
+        nc.sync.dma_start(shares[0 : 2 * BLOCKS : 2, :], lam[0, :].rearrange("(b c) -> b c", c=P))
+        nc.sync.dma_start(shares[1 : 2 * BLOCKS : 2, :], mu[0, :].rearrange("(b c) -> b c", c=P))
         for q in range(4):
             nc.sync.dma_start(xs[32 * q : 32 * q + 4, :].bitcast(I32), x_scales[0, 4 * q : 4 * q + 4, :].bitcast(I32))
         nc.sync.dma_start(xw[:], x_words[0].rearrange("p n t -> p (n t)").bitcast(I32))
         w_raw = []
         for c0, c1 in W_LOADS:
-            raw = keep.tile([P, 4, c1 - c0], F32, name="w_raw%d" % c0)
+            raw = tile("w_raw%d" % c0, [P, 4, c1 - c0], F32)
             nc.sync.dma_start(raw[:], w1[:, c0:c1].rearrange("(p j) c -> p j c", j=4))
-            for c in range(0, c1 - c0, P):
-                w_raw.append(raw[:, :, c : c + P].rearrange("p j (q u e) -> p q j u e", u=2, e=2))
+            w_raw.append(raw)
         nc.sync.dma_start(pos_sb[:], pos1)
-        nc.sync.dma_start(lam_rows[:], lam[:, SCALED_J0:SCALED_J1])
-        nc.sync.dma_start(mu_rows[:], mu[:, SCALED_J0:SCALED_J1])
         nc.sync.dma_start(w2w[:], w2_words[0].rearrange("p n t -> p (n t)").bitcast(I32))
         for q in range(4):
             nc.sync.dma_start(w2s[32 * q : 32 * q + 4, :].bitcast(I32), w2_scales[0, 4 * q : 4 * q + 4, :].bitcast(I32))
 
-        shares_turned = bank(BLOCKS - 1)
-        nc.tensor.transpose(shares_turned[:, 0:P], shares[:], ident[:])
-        lam_t = keep.tile([P, BLOCKS], F32, name="lam_t")
-        lam_first = keep.tile([P, 1], F32, name="lam_first", tag="late")
-        mu_t = keep.tile([P, BLOCKS], F32, name="mu_t")
-        nc.scalar.copy(lam_first[:], shares_turned[:, 0:1])
-        nc.scalar.copy(lam_t[:], shares_turned[:, 0:BLOCKS])
-        nc.scalar.copy(mu_t[:], shares_turned[:, BLOCKS : 2 * BLOCKS])
+        turned = bank(7)
+        nc.tensor.transpose(turned[:, 0:P], shares[:], ident[:])
+        num_view = turned[:, 0:18].rearrange("p (h x) -> p h x", h=2)[:, :, 0:8:2]
+        den_view = turned[:, 1:15].rearrange("p (h x) -> p h x", h=2)[:, :, 0:7:2]
+        num = tile("num", [P, BLOCKS], F32)
+        den = tile("den", [P, BLOCKS], F32)
+        size = tile("size", [P, BLOCKS], F32)
+        floor = tile("floor", [P, BLOCKS], F32)
+        side = tile("side", [P, BLOCKS], F32)
+        push = tile("push", [P, BLOCKS], F32)
+        outer_first = tile("outer_first", [P, BLOCKS], F32, tag="xg")
+        outer = tile("outer", [P, BLOCKS], F32)
+        inverse = tile("inverse", [P, BLOCKS], F32, tag="w_grouped0")
+        ratio = tile("ratio", [P, BLOCKS], F32)
+        nc.scalar.copy(den[:].rearrange("p (h x) -> p h x", h=2), den_view)
+        nc.scalar.activation(size[:].rearrange("p (h x) -> p h x", h=2), num_view, ABS, scale=2.0**-39)
+        nc.scalar.activation(floor[:], size[:], COPY, bias=2.0**-119)
+        nc.scalar.copy(num[:].rearrange("p (h x) -> p h x", h=2), num_view)
+        lam_last = tile("lam_last", [P, 1], F32, tag="early")
+        nc.scalar.copy(lam_last[:], turned[:, 10:11])
+        nc.gpsimd.tensor_scalar(side[:], den[:], 0.0, 0.5, IS_GE, SUB)
+        nc.gpsimd.tensor_tensor(push[:], floor[:], side[:], MULT)
+        nc.gpsimd.tensor_tensor(outer_first[:], den[:], push[:], ADD)
+        nc.gpsimd.tensor_tensor(outer[:], den[:], push[:], ADD)
 
-        xgs = keep.tile([P, S], U8, name="xgs", align_bytes=64)
+        xgs = tile("xgs", [P, S], U8)
         nc.vector.tensor_copy(xgs[:], xs[:].indirect(offs_sb[:]))
+        nc.vector.reciprocal(inverse[:], outer_first[:])
+        nc.gpsimd.tensor_tensor(ratio[:], num[:], inverse[:], MULT)
 
-        w_codes = keep.tile([P, H], U32, name="w_codes", align_bytes=64)
-        w_scales = keep.tile([P, H], U8, name="w_scales", align_bytes=64)
+        def spread(name, b0, n, b, tag):
+            acc = bank(b)
+            for k in range(n):
+                col = ratio[:, b0 + k : b0 + k + 1].to_broadcast([P, P])
+                nc.tensor.matmul(acc[:, k * P : (k + 1) * P], col, ident[:], start=True, stop=True, is_transpose=True)
+            rows = tile(name, [P, n * P], F32, tag=tag)
+            nc.scalar.copy(rows[:], acc[:, 0 : n * P])
+            return rows
 
-        def quantise_w(t):
-            last = t == TILES - 1
-            grouped = keep.tile(
-                [P, 2, 32, 2, 4], BF16, name="w_grouped%d" % t, tag="xw" if last else "w_grouped%d" % t, align_bytes=64
-            )
-            if last:
-                nc.vector.tensor_copy(grouped[:].rearrange("p u q e j -> p q j u e"), w_raw[t])
+        own_rows = spread("own_rows", 0, 4, 4, "late")
+
+        w_codes = tile("w_codes", [P, H], U32)
+        w_scales = [tile("w_scales0", [P, PAIR], U8), over_words("w_scales1", [P, PAIR], U8, 4096)]
+
+        def scales_of(c0, n):
+            return w_scales[c0 // PAIR][:, c0 % PAIR : c0 % PAIR + n]
+
+        def round_w(t):
+            raw = w_raw[min(t, 2)][:, :, (t // 3) * P : (t // 3 + 1) * P]
+            if t == 3:
+                grouped = over_words("w_grouped3", [P, P, 4], BF16, 0)
             else:
-                nc.scalar.copy(grouped[:].rearrange("p u q e j -> p q j u e"), w_raw[t])
+                grouped = tile("w_grouped%d" % t, [P, P, 4], BF16, tag=["w_grouped0", "w_raw0", "w_raw128"][t])
+            if t in (0, 3):
+                copy = nc.scalar.copy if t == 0 else nc.vector.tensor_copy
+                copy(grouped[:].rearrange("p (c i) j -> p c j i", i=4), raw.rearrange("p j (c i) -> p c j i", i=4))
+            else:
+                nc.gpsimd.tensor_scalar(grouped[:], raw.rearrange("p j c -> p c j"), 1.0, 0.0, MULT, ADD)
+            return grouped
+
+        def quantise_w(t, grouped):
             nc.vector.quantize_mx(
                 out=w_codes[:, t * P : (t + 1) * P].bitcast(FP8X4),
-                scales=w_scales[:, t * P : (t + 1) * P],
-                in_=grouped[:].rearrange("p u q e j -> p (u q e j)"),
+                scales=scales_of(t * P, P),
+                in_=grouped[:].rearrange("p c j -> p (c j)"),
             )
 
-        quantise_w(0)
-        xg = keep.tile([P, X_LAST], U32, name="xg", align_bytes=64)
-        xg_last = keep.tile([P, S - X_LAST], U32, name="xg_last", tag="w_grouped0", align_bytes=64)
+        xg = []
+        for k, (j0, n) in enumerate(X_PIECES):
+            words = tile("xg%d" % k, [P, n], U32, tag=["xg", "w_grouped0"][k])
+            nc.vector.tensor_copy(words[:], xw[:].bitcast(U32).indirect(entries(offs_sb, j0, n)))
+            xg.append(words)
+            quantise_w(k, round_w(k))
+        w_last = [round_w(2), round_w(3)]
+        quantise_w(2, w_last[0])
+        quantise_w(3, w_last[1])
 
         def picked(j0, n):
-            return xg[:, j0 : j0 + n] if j0 < X_LAST else xg_last[:, j0 - X_LAST : j0 - X_LAST + n]
-
-        for j0, n in X_PIECES:
-            nc.vector.tensor_copy(picked(j0, n), xw[:].bitcast(U32).indirect(entries(offs_sb, j0, n)))
-        quantise_w(1)
+            k = max(i for i, piece in enumerate(X_PIECES) if piece[0] <= j0)
+            return xg[k][:, j0 - X_PIECES[k][0] : j0 - X_PIECES[k][0] + n]
 
         def first_product(t, b, pieces, copy):
             acc = bank(b)
@@ -134,7 +174,7 @@ def tile_picked_mixup_none_p_kernel(
                 nc.tensor.matmul_mx(
                     out=acc[:, j0 - j_first : j0 - j_first + n],
                     lhsT=w_codes[:, t * P : (t + 1) * P].bitcast(FP8X4),
-                    lhsT_scale=w_scales[:, t * P : (t + 1) * P],
+                    lhsT_scale=scales_of(t * P, P),
                     rhs=picked(j0, n).bitcast(FP8X4),
                     rhs_scale=xgs[:, j0 : j0 + n],
                     start=True,
@@ -143,138 +183,103 @@ def tile_picked_mixup_none_p_kernel(
             width = sum(n for j0, n in pieces)
             copy(h[t][:, j_first : j_first + width], acc[:, 0:width])
 
-        h = [keep.tile([P, S], F32, name="h%d" % t) for t in range(TILES)]
+        h = [tile("h%d" % t, [P, S], F32) for t in range(TILES)]
         first_product(0, 0, X_PIECES[0:1], nc.scalar.copy)
-        first_product(0, 1, X_PIECES[1:2], nc.vector.tensor_copy)
-        first_product(0, BLOCKS - 1, X_PIECES[2:3], nc.scalar.copy)
+        partner_rows = spread("partner_rows", 6, 2, 6, None)
+        first_product(0, 1, X_PIECES[1:2], nc.scalar.copy)
         for t in range(1, TILES):
-            if t + 1 < TILES:
-                quantise_w(t + 1)
             first_product(t, 2 * t, X_PIECES[0:1], nc.scalar.copy)
-            first_product(t, 2 * t + 1, X_PIECES[1:3], nc.scalar.copy)
+            first_product(t, 2 * t + 1, X_PIECES[1:2], nc.scalar.copy)
 
         banks = [bank(b) for b in range(BLOCKS)]
-        partner = {}
-        own = {}
-        z_turned = {}
+        def by_halves(ap):
+            return ap.rearrange("p (q u e) -> p u q e", u=2, e=2)
 
-        def gather_partner(s, t, dst):
-            nc.vector.tensor_copy(dst, h[t][:].indirect(entries(pos_sb, s * HALF, HALF)))
-            partner[(s, t)] = dst
+        def in_places(ap):
+            return ap.rearrange("p (u q e) -> p u q e", u=2, e=2)
 
-        def turn_own(b, t):
-            turn(banks[b], t, h[t][:, b * P : (b + 1) * P])
-
-        def scale_own(b):
-            scaled = keep.tile([P, H], F32, name="own%d" % b)
-            if b in DIRECT:
+        mixed_own = {}
+        for b in (4, 5):
+            for c0 in (0, PAIR):
                 nc.tensor.matmul_mx(
-                    out=banks[b][:],
+                    out=banks[b][:, c0 : c0 + PAIR],
                     lhsT=picked(b * P, P).bitcast(FP8X4),
                     lhsT_scale=xgs[:, b * P : (b + 1) * P],
-                    rhs=w_codes[:].bitcast(FP8X4),
-                    rhs_scale=w_scales[:],
+                    rhs=w_codes[:, c0 : c0 + PAIR].bitcast(FP8X4),
+                    rhs_scale=scales_of(c0, PAIR),
                     start=True,
                     stop=True,
                 )
-                nc.scalar.activation(
-                    scaled[:].rearrange("p (u t x) -> p u t x", u=2, t=TILES),
-                    banks[b][:].rearrange("p (t u x) -> p u t x", u=2, t=TILES),
-                    COPY,
-                    scale=lam_t[:, b : b + 1],
-                )
-            else:
-                scale = lam_first[:] if b == 0 else lam_t[:, b : b + 1]
-                nc.scalar.activation(scaled[:], banks[b][:], COPY, scale=scale)
-            own[b] = scaled
+            mixed_own[b] = tile("mixed_own%d" % b, [P, H], F32)
+            scale = lam_last[:] if b == 5 else den[:, b : b + 1]
+            nc.scalar.activation(in_places(mixed_own[b][:]), by_halves(banks[b][:]), COPY, scale=scale)
             banks[b] = bank(b)
+        for t in range(TILES):
+            product = over_words("own0", [P, HALF], F32, 0) if t == 0 else tile("own%d" % t, [P, HALF], F32)
+            nc.gpsimd.tensor_tensor(product[:], h[t][:, 0:HALF], own_rows[:], MULT)
+            dst = tile("partner%d" % t, [P, HALF], F32)
+            nc.vector.tensor_copy(dst[:], h[t][:].indirect(entries(pos_sb, 0, HALF)))
+            for b in range(4):
+                turn(banks[b], t, product[:, b * P : (b + 1) * P], t == 0, False)
+                turn(banks[b], t, dst[:, b * P : (b + 1) * P], False, t == TILES - 1)
 
-        def add_product(name, t, values, factor, start, stop):
-            product = keep.tile(
-                [P, SCALED_J1 - SCALED_J0], F32, name="%s%d" % (name, t), tag="xw" if start else "%s%d" % (name, t), align_bytes=64
-            )
-            nc.gpsimd.tensor_tensor(product[:], values[:, SCALED_J0:SCALED_J1], factor[:], MULT)
-            for k, b in enumerate(SCALED):
-                turn(banks[b], t, product[:, k * P : (k + 1) * P], start=start, stop=stop)
+        for b in (6, 7):
+            for t in range(TILES):
+                turn(banks[b], t, h[t][:, b * P : (b + 1) * P], t == 0, False)
 
-        def add_own(t):
-            add_product("own_product", t, h[t], lam_rows, t == 0, False)
-
-        def add_partner(t):
-            add_product("partner_product", t, partner[(0, t)], mu_rows, False, t == TILES - 1)
-
-        def turn_partner(b, t):
-            s, c0 = divmod(b * P, HALF)
-            turn(banks[b], t, partner[(s, t)][:, c0 : c0 + P])
-
-        def mix(b):
-            z = keep.tile([P, H], BF16, name="z%d" % b)
-            if b in SCALED:
-                nc.scalar.copy(z[:], banks[b][:])
+        early = tile("partner_early", [P, 2, PAIR], F32, tag="early")
+        middle = tile("partner_middle", [P, PAIR], F32)
+        late = tile("partner_late", [P, TILES + 1, PAIR], F32, tag="late")
+        for t in range(TILES):
+            dst = [early[:, 0, :], early[:, 1, :], middle[:], late[:, TILES, :]][t]
+            window = h[t][:].indirect(entries(pos_sb, HALF, PAIR))
+            if t == 2:
+                nc.vector.tensor_copy(dst, window)
             else:
-                nc.vector.scalar_tensor_tensor(z[:], banks[b][:], mu_t[:, b : b + 1], own[b][:], MULT, ADD)
+                nc.scalar.activation(dst, window, COPY)
+            for k in range(2):
+                turn(banks[4 + k], t, dst[:, k * P : (k + 1) * P], True, True)
+
+        z_turned = {}
+        z_grouped = {}
+
+        def round_block(b, on_vector=False):
+            z = tile("z%d" % b, [P, H], BF16)
+            if on_vector:
+                nc.vector.tensor_scalar(in_places(z[:]), by_halves(banks[b][:]), outer[:, b : b + 1], None, MULT)
+            else:
+                nc.scalar.activation(in_places(z[:]), by_halves(banks[b][:]), COPY, scale=outer[:, b : b + 1])
             z_turned[b] = z
 
-        for t in range(TILES):
-            dst = keep.tile([P, HALF], F32, name="partner0%d" % t)
-            gather_partner(0, t, dst[:])
-        for t in range(2):
-            for b in MIXED:
-                if b not in DIRECT:
-                    turn_own(b, t)
-        for b in MIXED:
-            if b not in DIRECT:
-                turn_own(b, 2)
-                turn_own(b, 3)
-            scale_own(b)
-        late = keep.tile([P, TILES, HALF], F32, name="partner_late", tag="late")
-        gather_partner(1, 0, late[:, 0, :])
-        for t in range(1, TILES):
-            nc.vector.tensor_copy(late[:, t, 0:256], h[t][:].indirect(entries(pos_sb, HALF, 256)))
-            nc.scalar.activation(late[:, t, 256:512], h[t][:].indirect(entries(pos_sb, HALF + 256, 256)), COPY)
-            partner[(1, t)] = late[:, t, :]
+        def mix(b):
+            z = tile("z%d" % b, [P, H], BF16)
+            for u in range(2):
+                nc.vector.scalar_tensor_tensor(
+                    in_places(z[:])[:, u], by_halves(banks[b][:])[:, u], num[:, b : b + 1], in_places(mixed_own[b][:])[:, u], MULT, ADD
+                )
+            z_turned[b] = z
 
-        for t in range(2):
-            add_own(t)
-            add_partner(t)
-        for b in MIXED[:2]:
-            for t in range(3):
-                turn_partner(b, t)
-        add_own(2)
-        add_partner(2)
-        for b in MIXED[2:]:
-            turn_partner(b, 0)
-        add_own(3)
-        for b in MIXED[:2]:
-            turn_partner(b, 3)
-            mix(b)
-        add_partner(3)
-        for b in SCALED:
-            mix(b)
-        for b in MIXED[2:]:
-            for t in range(1, TILES):
-                turn_partner(b, t)
-            mix(b)
+        def turn_back(unit, k, copy):
+            b = unit[k]
+            if k == 0:
+                z_grouped[unit] = tile("z_grouped%d" % b, [P, len(unit) * P, 2], F32)
+            back = bank(b)
+            words = z_turned[b][:].bitcast(F32)
+            for u in range(2):
+                nc.tensor.transpose(back[:, u * P : (u + 1) * P], words[:, u * P : (u + 1) * P], ident[:])
+            copy(z_grouped[unit][:, k * P : (k + 1) * P, :], back[:, 0 : 2 * P].rearrange("p (u j) -> p j u", u=2))
 
-        z_grouped = []
-        for unit in UNITS:
-            grouped = keep.tile([P, len(unit) * P, 2], F32, name="z_grouped%d" % unit[0], align_bytes=64)
-            for k, b in enumerate(unit):
-                back = bank(b)
-                words = z_turned[b][:].bitcast(F32)
-                for u in range(2):
-                    nc.tensor.transpose(back[:, u * P : (u + 1) * P], words[:, u * P : (u + 1) * P], ident[:])
-                nc.scalar.copy(grouped[:, k * P : (k + 1) * P, :], back[:, 0 : 2 * P].rearrange("p (u j) -> p j u", u=2))
-            z_grouped.append(grouped)
+        z_codes = tile("z_codes", [P, S], U32)
 
-        z_codes = keep.tile([P, S], U32, name="z_codes", align_bytes=64)
-        for unit, grouped in zip(UNITS, z_grouped):
+        sums = {}
+
+        def second_product(unit):
             j0, n = unit[0] * P, len(unit) * P
-            z_scales = keep.tile([P, n], U8, name="z_scales%d" % unit[0], align_bytes=64)
+            z_scales = tile("z_scales%d" % unit[0], [P, n], U8)
             nc.vector.quantize_mx(
                 out=z_codes[:, j0 : j0 + n].bitcast(FP8X4),
                 scales=z_scales[:],
-                in_=grouped[:].rearrange("p j u -> p (j u)").bitcast(BF16),
+                in_=z_grouped[unit][:].rearrange("p j u -> p (j u)").bitcast(BF16),
             )
             acc = bank(unit[-1])
             nc.tensor.matmul_mx(
@@ -286,9 +291,32 @@ def tile_picked_mixup_none_p_kernel(
                 start=True,
                 stop=True,
             )
-            res = keep.tile([P, n], F32, name="res%d" % unit[0])
-            if len(unit) == 1:
-                nc.vector.tensor_copy(res[:], acc[:, 0:n])
-            else:
-                nc.scalar.copy(res[:], acc[:, 0:n])
+            sums[unit] = acc
+
+        def store(unit, copy):
+            j0, n = unit[0] * P, len(unit) * P
+            res = tile("res%d" % unit[0], [P, n], F32)
+            copy(res[:], sums[unit][:, 0:n])
             nc.sync.dma_start(out[:, j0 : j0 + n], res[:])
+
+        for t in range(TILES):
+            nc.vector.tensor_tensor(late[:, t, :], h[t][:].indirect(entries(pos_sb, 3 * PAIR, PAIR)), partner_rows[:], MULT)
+            for k in range(2):
+                turn(banks[6 + k], t, late[:, t, k * P : (k + 1) * P], False, t == TILES - 1)
+        for b in range(4):
+            round_block(b)
+        mix(4)
+        mix(5)
+        for unit in UNITS[0:2]:
+            for k in range(2):
+                turn_back(unit, k, nc.scalar.copy)
+        round_block(6, on_vector=True)
+        round_block(7, on_vector=True)
+        for k in range(2):
+            turn_back(UNITS[2], k, nc.scalar.copy)
+        turn_back(UNITS[3], 0, nc.scalar.copy)
+        turn_back(UNITS[4], 0, nc.scalar.copy)
+        for unit in UNITS:
+            second_product(unit)
+        for unit in UNITS:
+            store(unit, nc.scalar.copy if len(unit) == 2 else nc.vector.tensor_copy)

@@ -16,16 +16,16 @@ U8 = mybir.dt.uint8
 FP8X4 = mybir.dt.float8_e4m3fn_x4
 MULT = mybir.AluOpType.mult
 ADD = mybir.AluOpType.add
-SUB = mybir.AluOpType.subtract
-IS_GE = mybir.AluOpType.is_ge
+MAX = mybir.AluOpType.max
+MIN = mybir.AluOpType.min
 COPY = mybir.ActivationFunctionType.Copy
-ABS = mybir.ActivationFunctionType.Abs
 
 P = 128
 HALF = 512
 BLOCKS = S // P
 TILES = H // P
-X_PIECES = [(0, 512), (512, 512)]
+X_PIECES = [(0, 512), (512, 256), (768, 256)]
+X_LAST = X_PIECES[2][0]
 W_LOADS = [(0, 128), (128, 256), (256, 512)]
 UNITS = [(0, 1), (2, 3), (4, 5), (6,), (7,)]
 PAIR = 2 * P
@@ -37,29 +37,30 @@ def tile_picked_mixup_none_p_kernel(
     nc = tc.nc
     with ExitStack() as ctx:
         keep = ctx.enter_context(tc.tile_pool(name="keep", bufs=1))
-        reuse = ctx.enter_context(tc.tile_pool(name="reuse", bufs=1))
+        head = ctx.enter_context(tc.tile_pool(name="head", bufs=1))
         psum = ctx.enter_context(tc.psum_pool(name="psum", bufs=1))
 
         def bank(b):
             return psum.tile([P, HALF], F32, name="bank%d" % b, tag="bank%d" % b)
 
+        def block_bank(b):
+            return bank((b + 2) % BLOCKS)
+
         def tile(name, shape, dtype, tag=None):
             return keep.tile(shape, dtype, name=name, tag=tag or name, align_bytes=64)
-
-        def over_words(name, shape, dtype, offset):
-            return reuse.tile(shape, dtype, name=name, offset=offset, align_bytes=64)
 
         def entries(lst, j0, n):
             return lst[:, j0 // 16 : (j0 + n) // 16]
 
         def turn(dst_bank, t, src, start, stop):
-            nc.tensor.matmul(dst_bank[:, t * P : (t + 1) * P], src, ident[:], start=start, stop=stop, is_transpose=True)
+            dst = dst_bank[:].rearrange("p (u t x) -> p u t x", u=2, t=TILES)[:, :, t, :]
+            nc.tensor.matmul(dst, src, ident[:], start=start, stop=stop, is_transpose=True)
 
         offs_sb = keep.tile([P, S // 16], U16, name="offs_sb")
         pos_sb = keep.tile([P, S // 16], U16, name="pos_sb")
         xs = tile("xs", [P, T], U8)
-        xw = over_words("xw", [P, T], I32, 0)
-        shares = tile("shares", [P, P], F32)
+        xw = tile("xw", [P, T], I32)
+        shares = head.tile([P, P], F32, name="shares", offset=S - 256, align_bytes=64)
         w2w = tile("w2w", [P, N], I32)
         w2s = tile("w2s", [P, N], U8)
         ident = tile("ident", [P, P], F32)
@@ -70,9 +71,9 @@ def tile_picked_mixup_none_p_kernel(
         nc.vector.memset(ident[:], 0.0)
         make_identity(nc, ident[:], nomemset=True)
 
-        nc.sync.dma_start(offs_sb[:], offs)
         nc.sync.dma_start(shares[0 : 2 * BLOCKS : 2, :], lam[0, :].rearrange("(b c) -> b c", c=P))
         nc.sync.dma_start(shares[1 : 2 * BLOCKS : 2, :], mu[0, :].rearrange("(b c) -> b c", c=P))
+        nc.sync.dma_start(offs_sb[:], offs)
         for q in range(4):
             nc.sync.dma_start(xs[32 * q : 32 * q + 4, :].bitcast(I32), x_scales[0, 4 * q : 4 * q + 4, :].bitcast(I32))
         nc.sync.dma_start(xw[:], x_words[0].rearrange("p n t -> p (n t)").bitcast(I32))
@@ -80,7 +81,8 @@ def tile_picked_mixup_none_p_kernel(
         for c0, c1 in W_LOADS:
             raw = tile("w_raw%d" % c0, [P, 4, c1 - c0], F32)
             nc.sync.dma_start(raw[:], w1[:, c0:c1].rearrange("(p j) c -> p j c", j=4))
-            w_raw.append(raw)
+            for c in range(0, c1 - c0, P):
+                w_raw.append(raw[:, :, c : c + P].rearrange("p j (q u e) -> p q j u e", u=2, e=2))
         nc.sync.dma_start(pos_sb[:], pos1)
         nc.sync.dma_start(w2w[:], w2_words[0].rearrange("p n t -> p (n t)").bitcast(I32))
         for q in range(4):
@@ -92,29 +94,18 @@ def tile_picked_mixup_none_p_kernel(
         den_view = turned[:, 1:15].rearrange("p (h x) -> p h x", h=2)[:, :, 0:7:2]
         num = tile("num", [P, BLOCKS], F32)
         den = tile("den", [P, BLOCKS], F32)
-        size = tile("size", [P, BLOCKS], F32)
-        floor = tile("floor", [P, BLOCKS], F32)
-        side = tile("side", [P, BLOCKS], F32)
-        push = tile("push", [P, BLOCKS], F32)
-        outer_first = tile("outer_first", [P, BLOCKS], F32, tag="xg")
+        inverse = tile("inverse", [P, BLOCKS], F32)
+        bounded = tile("bounded", [P, BLOCKS], F32)
         outer = tile("outer", [P, BLOCKS], F32)
-        inverse = tile("inverse", [P, BLOCKS], F32, tag="w_grouped0")
-        ratio = tile("ratio", [P, BLOCKS], F32)
-        nc.scalar.copy(den[:].rearrange("p (h x) -> p h x", h=2), den_view)
-        nc.scalar.activation(size[:].rearrange("p (h x) -> p h x", h=2), num_view, ABS, scale=2.0**-39)
-        nc.scalar.activation(floor[:], size[:], COPY, bias=2.0**-119)
+        ratio = tile("ratio", [P, BLOCKS], F32, tag="w_grouped0")
+        nc.vector.reciprocal(inverse[:].rearrange("p (h x) -> p h x", h=2), den_view)
         nc.scalar.copy(num[:].rearrange("p (h x) -> p h x", h=2), num_view)
-        lam_last = tile("lam_last", [P, 1], F32, tag="early")
-        nc.scalar.copy(lam_last[:], turned[:, 10:11])
-        nc.gpsimd.tensor_scalar(side[:], den[:], 0.0, 0.5, IS_GE, SUB)
-        nc.gpsimd.tensor_tensor(push[:], floor[:], side[:], MULT)
-        nc.gpsimd.tensor_tensor(outer_first[:], den[:], push[:], ADD)
-        nc.gpsimd.tensor_tensor(outer[:], den[:], push[:], ADD)
+        nc.scalar.copy(den[:].rearrange("p (h x) -> p h x", h=2), den_view)
+        nc.gpsimd.tensor_scalar(bounded[:], inverse[:], -(2.0**60), 2.0**60, MAX, MIN)
+        nc.gpsimd.tensor_tensor(ratio[:], num[:], bounded[:], MULT)
 
-        xgs = tile("xgs", [P, S], U8)
+        xgs = head.tile([P, S], U8, name="xgs", offset=0, align_bytes=64)
         nc.vector.tensor_copy(xgs[:], xs[:].indirect(offs_sb[:]))
-        nc.vector.reciprocal(inverse[:], outer_first[:])
-        nc.gpsimd.tensor_tensor(ratio[:], num[:], inverse[:], MULT)
 
         def spread(name, b0, n, b, tag):
             acc = bank(b)
@@ -127,45 +118,32 @@ def tile_picked_mixup_none_p_kernel(
 
         own_rows = spread("own_rows", 0, 4, 4, "late")
 
+        partner_rows = spread("partner_rows", 6, 2, 6, None)
+
         w_codes = tile("w_codes", [P, H], U32)
-        w_scales = [tile("w_scales0", [P, PAIR], U8), over_words("w_scales1", [P, PAIR], U8, 4096)]
+        w_scales = tile("w_scales", [P, H], U8)
 
-        def scales_of(c0, n):
-            return w_scales[c0 // PAIR][:, c0 % PAIR : c0 % PAIR + n]
-
-        def round_w(t):
-            raw = w_raw[min(t, 2)][:, :, (t // 3) * P : (t // 3 + 1) * P]
-            if t == 3:
-                grouped = over_words("w_grouped3", [P, P, 4], BF16, 0)
-            else:
-                grouped = tile("w_grouped%d" % t, [P, P, 4], BF16, tag=["w_grouped0", "w_raw0", "w_raw128"][t])
-            if t in (0, 3):
-                copy = nc.scalar.copy if t == 0 else nc.vector.tensor_copy
-                copy(grouped[:].rearrange("p (c i) j -> p c j i", i=4), raw.rearrange("p j (c i) -> p c j i", i=4))
-            else:
-                nc.gpsimd.tensor_scalar(grouped[:], raw.rearrange("p j c -> p c j"), 1.0, 0.0, MULT, ADD)
-            return grouped
-
-        def quantise_w(t, grouped):
+        def quantise_w(t):
+            grouped = tile("w_grouped%d" % t, [P, 2, 32, 2, 4], BF16, tag=["w_grouped0", "w_raw0", "w_raw128", "xw"][t])
+            copy = nc.vector.tensor_copy if t == TILES - 1 else nc.scalar.copy
+            copy(grouped[:].rearrange("p u q e j -> p q j u e"), w_raw[t])
             nc.vector.quantize_mx(
                 out=w_codes[:, t * P : (t + 1) * P].bitcast(FP8X4),
-                scales=scales_of(t * P, P),
-                in_=grouped[:].rearrange("p c j -> p (c j)"),
+                scales=w_scales[:, t * P : (t + 1) * P],
+                in_=grouped[:].rearrange("p u q e j -> p (u q e j)"),
             )
 
-        xg = []
-        for k, (j0, n) in enumerate(X_PIECES):
-            words = tile("xg%d" % k, [P, n], U32, tag=["xg", "w_grouped0"][k])
-            nc.vector.tensor_copy(words[:], xw[:].bitcast(U32).indirect(entries(offs_sb, j0, n)))
-            xg.append(words)
-            quantise_w(k, round_w(k))
-        w_last = [round_w(2), round_w(3)]
-        quantise_w(2, w_last[0])
-        quantise_w(3, w_last[1])
+        quantise_w(0)
+        xg = head.tile([P, X_LAST], U32, name="xg", offset=S, align_bytes=64)
+        xg_last = tile("xg_last", [P, S - X_LAST], U32, tag="w_grouped0")
 
         def picked(j0, n):
-            k = max(i for i, piece in enumerate(X_PIECES) if piece[0] <= j0)
-            return xg[k][:, j0 - X_PIECES[k][0] : j0 - X_PIECES[k][0] + n]
+            return xg[:, j0 : j0 + n] if j0 < X_LAST else xg_last[:, j0 - X_LAST : j0 - X_LAST + n]
+
+        for j0, n in X_PIECES:
+            nc.vector.tensor_copy(picked(j0, n), xw[:].bitcast(U32).indirect(entries(offs_sb, j0, n)))
+        quantise_w(1)
+        nc.vector.reciprocal(outer[:], bounded[:])
 
         def first_product(t, b, pieces, copy):
             acc = bank(b)
@@ -174,7 +152,7 @@ def tile_picked_mixup_none_p_kernel(
                 nc.tensor.matmul_mx(
                     out=acc[:, j0 - j_first : j0 - j_first + n],
                     lhsT=w_codes[:, t * P : (t + 1) * P].bitcast(FP8X4),
-                    lhsT_scale=scales_of(t * P, P),
+                    lhsT_scale=w_scales[:, t * P : (t + 1) * P],
                     rhs=picked(j0, n).bitcast(FP8X4),
                     rhs_scale=xgs[:, j0 : j0 + n],
                     start=True,
@@ -185,37 +163,38 @@ def tile_picked_mixup_none_p_kernel(
 
         h = [tile("h%d" % t, [P, S], F32) for t in range(TILES)]
         first_product(0, 0, X_PIECES[0:1], nc.scalar.copy)
-        partner_rows = spread("partner_rows", 6, 2, 6, None)
-        first_product(0, 1, X_PIECES[1:2], nc.scalar.copy)
+        first_product(0, 1, X_PIECES[1:2], nc.vector.tensor_copy)
+        first_product(0, 7, X_PIECES[2:3], nc.scalar.copy)
         for t in range(1, TILES):
+            if t + 1 < TILES:
+                quantise_w(t + 1)
             first_product(t, 2 * t, X_PIECES[0:1], nc.scalar.copy)
-            first_product(t, 2 * t + 1, X_PIECES[1:2], nc.scalar.copy)
+            first_product(t, 2 * t + 1, X_PIECES[1:3], nc.scalar.copy)
 
-        banks = [bank(b) for b in range(BLOCKS)]
-        def by_halves(ap):
-            return ap.rearrange("p (q u e) -> p u q e", u=2, e=2)
-
-        def in_places(ap):
-            return ap.rearrange("p (u q e) -> p u q e", u=2, e=2)
-
+        banks = [block_bank(b) for b in range(BLOCKS)]
         mixed_own = {}
         for b in (4, 5):
-            for c0 in (0, PAIR):
-                nc.tensor.matmul_mx(
-                    out=banks[b][:, c0 : c0 + PAIR],
-                    lhsT=picked(b * P, P).bitcast(FP8X4),
-                    lhsT_scale=xgs[:, b * P : (b + 1) * P],
-                    rhs=w_codes[:, c0 : c0 + PAIR].bitcast(FP8X4),
-                    rhs_scale=scales_of(c0, PAIR),
-                    start=True,
-                    stop=True,
-                )
+            nc.tensor.matmul_mx(
+                out=banks[b][:],
+                lhsT=picked(b * P, P).bitcast(FP8X4),
+                lhsT_scale=xgs[:, b * P : (b + 1) * P],
+                rhs=w_codes[:].bitcast(FP8X4),
+                rhs_scale=w_scales[:],
+                start=True,
+                stop=True,
+            )
             mixed_own[b] = tile("mixed_own%d" % b, [P, H], F32)
-            scale = lam_last[:] if b == 5 else den[:, b : b + 1]
-            nc.scalar.activation(in_places(mixed_own[b][:]), by_halves(banks[b][:]), COPY, scale=scale)
-            banks[b] = bank(b)
+            nc.scalar.activation(
+                mixed_own[b][:].rearrange("p (u t x) -> p u t x", u=2, t=TILES),
+                banks[b][:].rearrange("p (t u x) -> p u t x", u=2, t=TILES),
+                COPY,
+                scale=den[:, b : b + 1],
+            )
+            banks[b] = block_bank(b)
         for t in range(TILES):
-            product = over_words("own0", [P, HALF], F32, 0) if t == 0 else tile("own%d" % t, [P, HALF], F32)
+            product = tile("own%d" % t, [P, HALF], F32, tag="xw" if t == 0 else None)
+            for b in (6, 7):
+                turn(banks[b], t, h[t][:, b * P : (b + 1) * P], t == 0, False)
             nc.gpsimd.tensor_tensor(product[:], h[t][:, 0:HALF], own_rows[:], MULT)
             dst = tile("partner%d" % t, [P, HALF], F32)
             nc.vector.tensor_copy(dst[:], h[t][:].indirect(entries(pos_sb, 0, HALF)))
@@ -223,20 +202,10 @@ def tile_picked_mixup_none_p_kernel(
                 turn(banks[b], t, product[:, b * P : (b + 1) * P], t == 0, False)
                 turn(banks[b], t, dst[:, b * P : (b + 1) * P], False, t == TILES - 1)
 
-        for b in (6, 7):
-            for t in range(TILES):
-                turn(banks[b], t, h[t][:, b * P : (b + 1) * P], t == 0, False)
-
-        early = tile("partner_early", [P, 2, PAIR], F32, tag="early")
-        middle = tile("partner_middle", [P, PAIR], F32)
         late = tile("partner_late", [P, TILES + 1, PAIR], F32, tag="late")
         for t in range(TILES):
-            dst = [early[:, 0, :], early[:, 1, :], middle[:], late[:, TILES, :]][t]
-            window = h[t][:].indirect(entries(pos_sb, HALF, PAIR))
-            if t == 2:
-                nc.vector.tensor_copy(dst, window)
-            else:
-                nc.scalar.activation(dst, window, COPY)
+            dst = late[:, TILES, :] if t == TILES - 1 else tile("partner_mixed%d" % t, [P, PAIR], F32)[:]
+            nc.scalar.activation(dst, h[t][:].indirect(entries(pos_sb, HALF, PAIR)), COPY)
             for k in range(2):
                 turn(banks[4 + k], t, dst[:, k * P : (k + 1) * P], True, True)
 
@@ -246,24 +215,21 @@ def tile_picked_mixup_none_p_kernel(
         def round_block(b, on_vector=False):
             z = tile("z%d" % b, [P, H], BF16)
             if on_vector:
-                nc.vector.tensor_scalar(in_places(z[:]), by_halves(banks[b][:]), outer[:, b : b + 1], None, MULT)
+                nc.vector.tensor_scalar(z[:], banks[b][:], outer[:, b : b + 1], None, MULT)
             else:
-                nc.scalar.activation(in_places(z[:]), by_halves(banks[b][:]), COPY, scale=outer[:, b : b + 1])
+                nc.scalar.activation(z[:], banks[b][:], COPY, scale=outer[:, b : b + 1])
             z_turned[b] = z
 
         def mix(b):
             z = tile("z%d" % b, [P, H], BF16)
-            for u in range(2):
-                nc.vector.scalar_tensor_tensor(
-                    in_places(z[:])[:, u], by_halves(banks[b][:])[:, u], num[:, b : b + 1], in_places(mixed_own[b][:])[:, u], MULT, ADD
-                )
+            nc.vector.scalar_tensor_tensor(z[:], banks[b][:], num[:, b : b + 1], mixed_own[b][:], MULT, ADD)
             z_turned[b] = z
 
         def turn_back(unit, k, copy):
             b = unit[k]
             if k == 0:
                 z_grouped[unit] = tile("z_grouped%d" % b, [P, len(unit) * P, 2], F32)
-            back = bank(b)
+            back = block_bank(b)
             words = z_turned[b][:].bitcast(F32)
             for u in range(2):
                 nc.tensor.transpose(back[:, u * P : (u + 1) * P], words[:, u * P : (u + 1) * P], ident[:])
@@ -281,7 +247,7 @@ def tile_picked_mixup_none_p_kernel(
                 scales=z_scales[:],
                 in_=z_grouped[unit][:].rearrange("p j u -> p (j u)").bitcast(BF16),
             )
-            acc = bank(unit[-1])
+            acc = block_bank(unit[-1])
             nc.tensor.matmul_mx(
                 out=acc[:, 0:n],
                 lhsT=w2w[:].bitcast(FP8X4),
@@ -319,4 +285,4 @@ def tile_picked_mixup_none_p_kernel(
         for unit in UNITS:
             second_product(unit)
         for unit in UNITS:
-            store(unit, nc.scalar.copy if len(unit) == 2 else nc.vector.tensor_copy)
+            store(unit, nc.scalar.copy if unit[0] < 4 else nc.vector.tensor_copy)

@@ -123,17 +123,22 @@ def tile_picked_mixup_none_p_kernel(
         w_codes = tile("w_codes", [P, H], U32)
         w_scales = tile("w_scales", [P, H], U8)
 
-        def quantise_w(t):
-            grouped = tile("w_grouped%d" % t, [P, 2, 32, 2, 4], BF16, tag=["w_grouped0", "w_raw0", "w_raw128", "xw"][t])
-            copy = nc.vector.tensor_copy if t == TILES - 1 else nc.scalar.copy
-            copy(grouped[:].rearrange("p u q e j -> p q j u e"), w_raw[t])
+        def round_w(t, grouped):
+            copy = nc.scalar.copy if t < 2 else nc.vector.tensor_copy
+            copy(grouped.rearrange("p u q e j -> p q j u e"), w_raw[t])
+
+        def quantise_w(t, grouped):
+            n = grouped.shape[1] * P
             nc.vector.quantize_mx(
-                out=w_codes[:, t * P : (t + 1) * P].bitcast(FP8X4),
-                scales=w_scales[:, t * P : (t + 1) * P],
-                in_=grouped[:].rearrange("p u q e j -> p (u q e j)"),
+                out=w_codes[:, t * P : t * P + n].bitcast(FP8X4),
+                scales=w_scales[:, t * P : t * P + n],
+                in_=grouped[:].rearrange("p t u q e j -> p (t u q e j)"),
             )
 
-        quantise_w(0)
+        w_grouped = [tile("w_grouped%d" % t, [P, 1, 2, 32, 2, 4], BF16, tag=["w_grouped0", "w_raw0"][t]) for t in range(2)]
+        for t in range(2):
+            round_w(t, w_grouped[t][:, 0])
+        quantise_w(0, w_grouped[0])
         xg = head.tile([P, X_LAST], U32, name="xg", offset=S, align_bytes=64)
         xg_last = tile("xg_last", [P, S - X_LAST], U32, tag="w_grouped0")
 
@@ -142,8 +147,11 @@ def tile_picked_mixup_none_p_kernel(
 
         for j0, n in X_PIECES:
             nc.vector.tensor_copy(picked(j0, n), xw[:].bitcast(U32).indirect(entries(offs_sb, j0, n)))
-        quantise_w(1)
+        quantise_w(1, w_grouped[1])
         nc.vector.reciprocal(outer[:], bounded[:])
+        w_last = tile("w_last", [P, 2, 2, 32, 2, 4], BF16, tag="xw")
+        for t in (2, 3):
+            round_w(t, w_last[:, t - 2])
 
         def first_product(t, b, pieces, copy):
             acc = bank(b)
@@ -165,9 +173,8 @@ def tile_picked_mixup_none_p_kernel(
         first_product(0, 0, X_PIECES[0:1], nc.scalar.copy)
         first_product(0, 1, X_PIECES[1:2], nc.vector.tensor_copy)
         first_product(0, 7, X_PIECES[2:3], nc.scalar.copy)
+        quantise_w(2, w_last)
         for t in range(1, TILES):
-            if t + 1 < TILES:
-                quantise_w(t + 1)
             first_product(t, 2 * t, X_PIECES[0:1], nc.scalar.copy)
             first_product(t, 2 * t + 1, X_PIECES[1:3], nc.scalar.copy)
 

@@ -27,8 +27,10 @@ TILES = H // P
 X_PIECES = [(0, 512), (512, 256), (768, 256)]
 X_LAST = X_PIECES[2][0]
 W_LOADS = [(0, 128), (128, 256), (256, 512)]
-UNITS = [(0, 1), (2, 3), (4, 5), (6,), (7,)]
+UNITS = [(0, 1), (2, 3), (6, 7), (4,), (5,)]
 PAIR = 2 * P
+RATIO = 6
+MIXED = range(RATIO, BLOCKS)
 
 
 def tile_picked_mixup_none_p_kernel(
@@ -44,7 +46,7 @@ def tile_picked_mixup_none_p_kernel(
             return psum.tile([P, HALF], F32, name="bank%d" % b, tag="bank%d" % b)
 
         def block_bank(b):
-            return bank((b + 2) % BLOCKS)
+            return bank(b)
 
         def tile(name, shape, dtype, tag=None):
             return keep.tile(shape, dtype, name=name, tag=tag or name, align_bytes=64)
@@ -71,8 +73,8 @@ def tile_picked_mixup_none_p_kernel(
         nc.vector.memset(ident[:], 0.0)
         make_identity(nc, ident[:], nomemset=True)
 
-        nc.sync.dma_start(shares[0 : 2 * BLOCKS : 2, :], lam[0, :].rearrange("(b c) -> b c", c=P))
-        nc.sync.dma_start(shares[1 : 2 * BLOCKS : 2, :], mu[0, :].rearrange("(b c) -> b c", c=P))
+        nc.sync.dma_start(shares[0:BLOCKS, :], lam[0, :].rearrange("(b c) -> b c", c=P))
+        nc.sync.dma_start(shares[BLOCKS : 2 * BLOCKS, :], mu[0, :].rearrange("(b c) -> b c", c=P))
         nc.sync.dma_start(offs_sb[:], offs)
         for q in range(4):
             nc.sync.dma_start(xs[32 * q : 32 * q + 4, :].bitcast(I32), x_scales[0, 4 * q : 4 * q + 4, :].bitcast(I32))
@@ -90,19 +92,15 @@ def tile_picked_mixup_none_p_kernel(
 
         turned = bank(7)
         nc.tensor.transpose(turned[:, 0:P], shares[:], ident[:])
-        num_view = turned[:, 0:18].rearrange("p (h x) -> p h x", h=2)[:, :, 0:8:2]
-        den_view = turned[:, 1:15].rearrange("p (h x) -> p h x", h=2)[:, :, 0:7:2]
-        num = tile("num", [P, BLOCKS], F32)
-        den = tile("den", [P, BLOCKS], F32)
-        inverse = tile("inverse", [P, BLOCKS], F32)
-        bounded = tile("bounded", [P, BLOCKS], F32)
-        outer = tile("outer", [P, BLOCKS], F32)
-        ratio = tile("ratio", [P, BLOCKS], F32, tag="w_grouped0")
-        nc.vector.reciprocal(inverse[:].rearrange("p (h x) -> p h x", h=2), den_view)
-        nc.scalar.copy(num[:].rearrange("p (h x) -> p h x", h=2), num_view)
-        nc.scalar.copy(den[:].rearrange("p (h x) -> p h x", h=2), den_view)
+        lam_mu = tile("lam_mu", [P, 2 * BLOCKS], F32)
+        inverse = tile("inverse", [P, RATIO], F32)
+        bounded = tile("bounded", [P, RATIO], F32)
+        outer = tile("outer", [P, RATIO], F32)
+        ratio = tile("ratio", [P, RATIO], F32, tag="w_grouped0")
+        nc.vector.reciprocal(inverse[:], turned[:, 0:RATIO])
+        nc.scalar.copy(lam_mu[:], turned[:, 0 : 2 * BLOCKS])
         nc.gpsimd.tensor_scalar(bounded[:], inverse[:], -(2.0**60), 2.0**60, MAX, MIN)
-        nc.gpsimd.tensor_tensor(ratio[:], num[:], bounded[:], MULT)
+        nc.gpsimd.tensor_tensor(ratio[:], lam_mu[:, BLOCKS : BLOCKS + RATIO], bounded[:], MULT)
 
         xgs = head.tile([P, S], U8, name="xgs", offset=0, align_bytes=64)
         nc.vector.tensor_copy(xgs[:], xs[:].indirect(offs_sb[:]))
@@ -116,9 +114,9 @@ def tile_picked_mixup_none_p_kernel(
             nc.scalar.copy(rows[:], acc[:, 0 : n * P])
             return rows
 
-        own_rows = spread("own_rows", 0, 4, 4, "late")
+        rows_early = spread("rows_early", 0, 4, 4, None)
 
-        partner_rows = spread("partner_rows", 6, 2, 6, None)
+        rows_late = spread("rows_late", 4, RATIO - 4, 6, None)
 
         w_codes = tile("w_codes", [P, H], U32)
         w_scales = tile("w_scales", [P, H], U8)
@@ -180,7 +178,7 @@ def tile_picked_mixup_none_p_kernel(
 
         banks = [block_bank(b) for b in range(BLOCKS)]
         mixed_own = {}
-        for b in (4, 5):
+        for b in MIXED:
             nc.tensor.matmul_mx(
                 out=banks[b][:],
                 lhsT=picked(b * P, P).bitcast(FP8X4),
@@ -195,26 +193,29 @@ def tile_picked_mixup_none_p_kernel(
                 mixed_own[b][:].rearrange("p (u t x) -> p u t x", u=2, t=TILES),
                 banks[b][:].rearrange("p (t u x) -> p u t x", u=2, t=TILES),
                 COPY,
-                scale=den[:, b : b + 1],
+                scale=lam_mu[:, b : b + 1],
             )
             banks[b] = block_bank(b)
         for t in range(TILES):
-            product = tile("own%d" % t, [P, HALF], F32, tag="xw" if t == 0 else None)
-            for b in (6, 7):
+            for b in range(RATIO):
                 turn(banks[b], t, h[t][:, b * P : (b + 1) * P], t == 0, False)
-            nc.gpsimd.tensor_tensor(product[:], h[t][:, 0:HALF], own_rows[:], MULT)
             dst = tile("partner%d" % t, [P, HALF], F32)
-            nc.vector.tensor_copy(dst[:], h[t][:].indirect(entries(pos_sb, 0, HALF)))
+            nc.vector.tensor_tensor(dst[:], h[t][:].indirect(entries(pos_sb, 0, HALF)), rows_early[:], MULT)
             for b in range(4):
-                turn(banks[b], t, product[:, b * P : (b + 1) * P], t == 0, False)
                 turn(banks[b], t, dst[:, b * P : (b + 1) * P], False, t == TILES - 1)
 
-        late = tile("partner_late", [P, TILES + 1, PAIR], F32, tag="late")
+        n_late = (RATIO - 4) * P
+        n_mixed = len(MIXED) * P
+        late = tile("partner_late", [P, TILES, n_late], F32, tag="w_grouped0")
         for t in range(TILES):
-            dst = late[:, TILES, :] if t == TILES - 1 else tile("partner_mixed%d" % t, [P, PAIR], F32)[:]
-            nc.scalar.activation(dst, h[t][:].indirect(entries(pos_sb, HALF, PAIR)), COPY)
-            for k in range(2):
-                turn(banks[4 + k], t, dst[:, k * P : (k + 1) * P], True, True)
+            dst = tile("partner_mixed%d" % t, [P, n_mixed], F32)
+            window = h[t][:].indirect(entries(pos_sb, RATIO * P, n_mixed))
+            if t == TILES - 1:
+                nc.vector.tensor_copy(dst[:], window)
+            else:
+                nc.scalar.activation(dst[:], window, COPY)
+            for k, b in enumerate(MIXED):
+                turn(banks[b], t, dst[:, k * P : (k + 1) * P], True, True)
 
         z_turned = {}
         z_grouped = {}
@@ -229,7 +230,7 @@ def tile_picked_mixup_none_p_kernel(
 
         def mix(b):
             z = tile("z%d" % b, [P, H], BF16)
-            nc.vector.scalar_tensor_tensor(z[:], banks[b][:], num[:, b : b + 1], mixed_own[b][:], MULT, ADD)
+            nc.vector.scalar_tensor_tensor(z[:], banks[b][:], lam_mu[:, BLOCKS + b : BLOCKS + b + 1], mixed_own[b][:], MULT, ADD)
             z_turned[b] = z
 
         def turn_back(unit, k, copy):
@@ -273,18 +274,18 @@ def tile_picked_mixup_none_p_kernel(
             nc.sync.dma_start(out[:, j0 : j0 + n], res[:])
 
         for t in range(TILES):
-            nc.vector.tensor_tensor(late[:, t, :], h[t][:].indirect(entries(pos_sb, 3 * PAIR, PAIR)), partner_rows[:], MULT)
-            for k in range(2):
-                turn(banks[6 + k], t, late[:, t, k * P : (k + 1) * P], False, t == TILES - 1)
+            nc.vector.tensor_tensor(late[:, t, :], h[t][:].indirect(entries(pos_sb, HALF, n_late)), rows_late[:], MULT)
+            for b in range(4, RATIO):
+                turn(banks[b], t, late[:, t, (b - 4) * P : (b - 3) * P], False, t == TILES - 1)
         for b in range(4):
             round_block(b)
-        mix(4)
-        mix(5)
+        mix(6)
+        mix(7)
         for unit in UNITS[0:2]:
             for k in range(2):
                 turn_back(unit, k, nc.scalar.copy)
-        round_block(6, on_vector=True)
-        round_block(7, on_vector=True)
+        round_block(4, on_vector=True)
+        round_block(5, on_vector=True)
         for k in range(2):
             turn_back(UNITS[2], k, nc.scalar.copy)
         turn_back(UNITS[3], 0, nc.scalar.copy)
@@ -292,4 +293,4 @@ def tile_picked_mixup_none_p_kernel(
         for unit in UNITS:
             second_product(unit)
         for unit in UNITS:
-            store(unit, nc.scalar.copy if unit[0] < 4 else nc.vector.tensor_copy)
+            store(unit, nc.vector.tensor_copy if unit[0] == 5 else nc.scalar.copy)

@@ -18,6 +18,8 @@ MULT = mybir.AluOpType.mult
 ADD = mybir.AluOpType.add
 MAX = mybir.AluOpType.max
 MIN = mybir.AluOpType.min
+SUB = mybir.AluOpType.subtract
+IS_GE = mybir.AluOpType.is_ge
 COPY = mybir.ActivationFunctionType.Copy
 
 P = 128
@@ -102,21 +104,24 @@ def tile_picked_mixup_none_p_kernel(
         nc.gpsimd.tensor_scalar(bounded[:], inverse[:], -(2.0**60), 2.0**60, MAX, MIN)
         nc.gpsimd.tensor_tensor(ratio[:], lam_mu[:, BLOCKS : BLOCKS + RATIO], bounded[:], MULT)
 
+        side = tile("side", [P, RATIO], F32)
+        half_size = tile("half_size", [P, RATIO], F32)
+        twice_size = tile("twice_size", [P, RATIO], F32)
+        nc.gpsimd.tensor_scalar(side[:], inverse[:], 0.0, 0.5, IS_GE, SUB)
+        nc.gpsimd.tensor_tensor(half_size[:], lam_mu[:, 0:RATIO], side[:], MULT)
+        nc.gpsimd.tensor_scalar(twice_size[:], half_size[:], 2.0**-61, 4.0, MAX, MULT)
+        nc.gpsimd.tensor_tensor(outer[:], twice_size[:], side[:], MULT)
+
         xgs = head.tile([P, S], U8, name="xgs", offset=0, align_bytes=64)
         nc.vector.tensor_copy(xgs[:], xs[:].indirect(offs_sb[:]))
 
-        def spread(name, b0, n, b, tag):
+        rows = tile("rows", [P, RATIO * P], F32)
+        for b0, n, b in ((0, 4, 4), (4, RATIO - 4, 6)):
             acc = bank(b)
             for k in range(n):
                 col = ratio[:, b0 + k : b0 + k + 1].to_broadcast([P, P])
                 nc.tensor.matmul(acc[:, k * P : (k + 1) * P], col, ident[:], start=True, stop=True, is_transpose=True)
-            rows = tile(name, [P, n * P], F32, tag=tag)
-            nc.scalar.copy(rows[:], acc[:, 0 : n * P])
-            return rows
-
-        rows_early = spread("rows_early", 0, 4, 4, None)
-
-        rows_late = spread("rows_late", 4, RATIO - 4, 6, None)
+            nc.scalar.copy(rows[:, b0 * P : (b0 + n) * P], acc[:, 0 : n * P])
 
         w_codes = tile("w_codes", [P, H], U32)
         w_scales = tile("w_scales", [P, H], U8)
@@ -143,10 +148,9 @@ def tile_picked_mixup_none_p_kernel(
         def picked(j0, n):
             return xg[:, j0 : j0 + n] if j0 < X_LAST else xg_last[:, j0 - X_LAST : j0 - X_LAST + n]
 
-        for j0, n in X_PIECES:
+        for j0, n in ((0, X_LAST), (X_LAST, S - X_LAST)):
             nc.vector.tensor_copy(picked(j0, n), xw[:].bitcast(U32).indirect(entries(offs_sb, j0, n)))
         quantise_w(1, w_grouped[1])
-        nc.vector.reciprocal(outer[:], bounded[:])
         w_last = tile("w_last", [P, 2, 2, 32, 2, 4], BF16, tag="xw")
         for t in (2, 3):
             round_w(t, w_last[:, t - 2])
@@ -199,9 +203,10 @@ def tile_picked_mixup_none_p_kernel(
         for t in range(TILES):
             for b in range(RATIO):
                 turn(banks[b], t, h[t][:, b * P : (b + 1) * P], t == 0, False)
-            dst = tile("partner%d" % t, [P, HALF], F32)
-            nc.vector.tensor_tensor(dst[:], h[t][:].indirect(entries(pos_sb, 0, HALF)), rows_early[:], MULT)
-            for b in range(4):
+            n = 4
+            dst = tile("partner%d" % t, [P, n * P], F32)
+            nc.vector.tensor_tensor(dst[:], h[t][:].indirect(entries(pos_sb, 0, n * P)), rows[:, 0 : n * P], MULT)
+            for b in range(n):
                 turn(banks[b], t, dst[:, b * P : (b + 1) * P], False, t == TILES - 1)
 
         n_late = (RATIO - 4) * P
@@ -209,11 +214,11 @@ def tile_picked_mixup_none_p_kernel(
         late = tile("partner_late", [P, TILES, n_late], F32, tag="w_grouped0")
         for t in range(TILES):
             dst = tile("partner_mixed%d" % t, [P, n_mixed], F32)
-            window = h[t][:].indirect(entries(pos_sb, RATIO * P, n_mixed))
             if t == TILES - 1:
-                nc.vector.tensor_copy(dst[:], window)
+                nc.vector.tensor_copy(dst[:, 0:P], h[t][:].indirect(entries(pos_sb, RATIO * P, P)))
+                nc.scalar.activation(dst[:, P:PAIR], h[t][:].indirect(entries(pos_sb, RATIO * P + P, P)), COPY)
             else:
-                nc.scalar.activation(dst[:], window, COPY)
+                nc.scalar.activation(dst[:], h[t][:].indirect(entries(pos_sb, RATIO * P, n_mixed)), COPY)
             for k, b in enumerate(MIXED):
                 turn(banks[b], t, dst[:, k * P : (k + 1) * P], True, True)
 
@@ -274,7 +279,7 @@ def tile_picked_mixup_none_p_kernel(
             nc.sync.dma_start(out[:, j0 : j0 + n], res[:])
 
         for t in range(TILES):
-            nc.vector.tensor_tensor(late[:, t, :], h[t][:].indirect(entries(pos_sb, HALF, n_late)), rows_late[:], MULT)
+            nc.vector.tensor_tensor(late[:, t, :], h[t][:].indirect(entries(pos_sb, HALF, n_late)), rows[:, HALF:], MULT)
             for b in range(4, RATIO):
                 turn(banks[b], t, late[:, t, (b - 4) * P : (b - 3) * P], False, t == TILES - 1)
         for b in range(4):
@@ -293,4 +298,4 @@ def tile_picked_mixup_none_p_kernel(
         for unit in UNITS:
             second_product(unit)
         for unit in UNITS:
-            store(unit, nc.vector.tensor_copy if unit[0] == 5 else nc.scalar.copy)
+            store(unit, nc.vector.tensor_copy if len(unit) == 1 else nc.scalar.copy)

@@ -21,6 +21,7 @@ MIN = mybir.AluOpType.min
 SUB = mybir.AluOpType.subtract
 IS_GE = mybir.AluOpType.is_ge
 COPY = mybir.ActivationFunctionType.Copy
+ABS = mybir.ActivationFunctionType.Abs
 
 P = 128
 HALF = 512
@@ -101,15 +102,25 @@ def tile_picked_mixup_none_p_kernel(
         ratio = tile("ratio", [P, RATIO], F32, tag="w_grouped0")
         nc.vector.reciprocal(inverse[:], turned[:, 0:RATIO])
         nc.scalar.copy(lam_mu[:], turned[:, 0 : 2 * BLOCKS])
-        nc.gpsimd.tensor_scalar(bounded[:], inverse[:], -(2.0**60), 2.0**60, MAX, MIN)
-        nc.gpsimd.tensor_tensor(ratio[:], lam_mu[:, BLOCKS : BLOCKS + RATIO], bounded[:], MULT)
+        floor = tile("floor", [P, RATIO], F32)
+        nc.scalar.activation(floor[:], turned[:, BLOCKS : BLOCKS + RATIO], ABS, scale=2.0**-41)
+        quotient = tile("quotient", [P, RATIO], F32)
+        nc.gpsimd.tensor_scalar(bounded[:], inverse[:], -(2.0**120), 2.0**120, MAX, MIN)
+        nc.gpsimd.tensor_tensor(quotient[:], lam_mu[:, BLOCKS : BLOCKS + RATIO], bounded[:], MULT)
+        nc.gpsimd.tensor_scalar(ratio[:], quotient[:], -(2.0**40), 2.0**40, MAX, MIN)
 
         side = tile("side", [P, RATIO], F32)
         half_size = tile("half_size", [P, RATIO], F32)
+        excess = tile("excess", [P, RATIO], F32)
+        above = tile("above", [P, RATIO], F32)
+        larger = tile("larger", [P, RATIO], F32)
         twice_size = tile("twice_size", [P, RATIO], F32)
         nc.gpsimd.tensor_scalar(side[:], inverse[:], 0.0, 0.5, IS_GE, SUB)
         nc.gpsimd.tensor_tensor(half_size[:], lam_mu[:, 0:RATIO], side[:], MULT)
-        nc.gpsimd.tensor_scalar(twice_size[:], half_size[:], 2.0**-61, 4.0, MAX, MULT)
+        nc.gpsimd.tensor_tensor(excess[:], half_size[:], floor[:], SUB)
+        nc.gpsimd.tensor_scalar(above[:], excess[:], 0.0, 1.0, MAX, MULT)
+        nc.gpsimd.tensor_tensor(larger[:], floor[:], above[:], ADD)
+        nc.gpsimd.tensor_scalar(twice_size[:], larger[:], 2.0**-121, 4.0, MAX, MULT)
         nc.gpsimd.tensor_tensor(outer[:], twice_size[:], side[:], MULT)
 
         xgs = head.tile([P, S], U8, name="xgs", offset=0, align_bytes=64)

@@ -49,7 +49,7 @@ def tile_picked_mixup_none_p_kernel(
             return psum.tile([P, HALF], F32, name="bank%d" % b, tag="bank%d" % b)
 
         def block_bank(b):
-            return bank(b)
+            return bank([0, 1, 2, 3, 5, 6, 7, 4][b])
 
         def tile(name, shape, dtype, tag=None):
             return keep.tile(shape, dtype, name=name, tag=tag or name, align_bytes=64)
@@ -93,7 +93,7 @@ def tile_picked_mixup_none_p_kernel(
         for q in range(4):
             nc.sync.dma_start(w2s[32 * q : 32 * q + 4, :].bitcast(I32), w2_scales[0, 4 * q : 4 * q + 4, :].bitcast(I32))
 
-        turned = bank(7)
+        turned = bank(2)
         nc.tensor.transpose(turned[:, 0:P], shares[:], ident[:])
         lam_mu = tile("lam_mu", [P, 2 * BLOCKS], F32)
         inverse = tile("inverse", [P, RATIO], F32)
@@ -127,7 +127,7 @@ def tile_picked_mixup_none_p_kernel(
         nc.vector.tensor_copy(xgs[:], xs[:].indirect(offs_sb[:]))
 
         rows = tile("rows", [P, RATIO * P], F32)
-        for b0, n, b in ((0, 4, 4), (4, RATIO - 4, 6)):
+        for b0, n, b in ((0, 4, 0), (4, RATIO - 4, 1)):
             acc = bank(b)
             for k in range(n):
                 col = ratio[:, b0 + k : b0 + k + 1].to_broadcast([P, P])
@@ -183,13 +183,13 @@ def tile_picked_mixup_none_p_kernel(
             copy(h[t][:, j_first : j_first + width], acc[:, 0:width])
 
         h = [tile("h%d" % t, [P, S], F32) for t in range(TILES)]
-        first_product(0, 0, X_PIECES[0:1], nc.scalar.copy)
-        first_product(0, 1, X_PIECES[1:2], nc.vector.tensor_copy)
-        first_product(0, 7, X_PIECES[2:3], nc.scalar.copy)
+        first_product(0, 4, X_PIECES[0:1], nc.scalar.copy)
+        first_product(0, 5, X_PIECES[1:2], nc.vector.tensor_copy)
+        first_product(0, 6, X_PIECES[2:3], nc.scalar.copy)
         quantise_w(2, w_last)
         for t in range(1, TILES):
-            first_product(t, 2 * t, X_PIECES[0:1], nc.scalar.copy)
-            first_product(t, 2 * t + 1, X_PIECES[1:3], nc.scalar.copy)
+            first_product(t, 4 + (2 * t + 1) % 4, X_PIECES[0:1], nc.scalar.copy)
+            first_product(t, 4 + (2 * t + 2) % 4, X_PIECES[1:3], nc.scalar.copy)
 
         banks = [block_bank(b) for b in range(BLOCKS)]
         mixed_own = {}
@@ -249,15 +249,20 @@ def tile_picked_mixup_none_p_kernel(
             nc.vector.scalar_tensor_tensor(z[:], banks[b][:], lam_mu[:, BLOCKS + b : BLOCKS + b + 1], mixed_own[b][:], MULT, ADD)
             z_turned[b] = z
 
-        def turn_back(unit, k, copy):
-            b = unit[k]
-            if k == 0:
-                z_grouped[unit] = tile("z_grouped%d" % b, [P, len(unit) * P, 2], F32)
-            back = block_bank(b)
+        backs = {}
+
+        def turn_back(b):
+            backs[b] = block_bank(b)
             words = z_turned[b][:].bitcast(F32)
             for u in range(2):
-                nc.tensor.transpose(back[:, u * P : (u + 1) * P], words[:, u * P : (u + 1) * P], ident[:])
-            copy(z_grouped[unit][:, k * P : (k + 1) * P, :], back[:, 0 : 2 * P].rearrange("p (u j) -> p j u", u=2))
+                nc.tensor.transpose(backs[b][:, u * P : (u + 1) * P], words[:, u * P : (u + 1) * P], ident[:])
+
+        def group(unit):
+            z_grouped[unit] = tile("z_grouped%d" % unit[0], [P, len(unit) * P, 2], F32)
+            for k, b in enumerate(unit):
+                nc.scalar.copy(
+                    z_grouped[unit][:, k * P : (k + 1) * P, :], backs[b][:, 0 : 2 * P].rearrange("p (u j) -> p j u", u=2)
+                )
 
         z_codes = tile("z_codes", [P, S], U32)
 
@@ -289,23 +294,31 @@ def tile_picked_mixup_none_p_kernel(
             copy(res[:], sums[unit][:, 0:n])
             nc.sync.dma_start(out[:, j0 : j0 + n], res[:])
 
-        for t in range(TILES):
+        def late_partner(t):
             nc.vector.tensor_tensor(late[:, t, :], h[t][:].indirect(entries(pos_sb, HALF, n_late)), rows[:, HALF:], MULT)
             for b in range(4, RATIO):
                 turn(banks[b], t, late[:, t, (b - 4) * P : (b - 3) * P], False, t == TILES - 1)
+
+        late_partner(0)
+        late_partner(1)
         for b in range(4):
             round_block(b)
+        turn_back(0)
+        late_partner(2)
+        turn_back(1)
+        late_partner(3)
+        turn_back(2)
+        turn_back(3)
         mix(6)
         mix(7)
-        for unit in UNITS[0:2]:
-            for k in range(2):
-                turn_back(unit, k, nc.scalar.copy)
+        group(UNITS[0])
+        group(UNITS[1])
         round_block(4, on_vector=True)
         round_block(5, on_vector=True)
-        for k in range(2):
-            turn_back(UNITS[2], k, nc.scalar.copy)
-        turn_back(UNITS[3], 0, nc.scalar.copy)
-        turn_back(UNITS[4], 0, nc.scalar.copy)
+        for unit in UNITS[2:]:
+            for b in unit:
+                turn_back(b)
+            group(unit)
         for unit in UNITS:
             second_product(unit)
         for unit in UNITS:

from contextlib import ExitStack

import concourse.mybir as mybir
from concourse.masks import make_identity

K, T, S, H, N = 512, 2048, 1024, 512, 128
FLOPS = 2 * K * H * S + 2 * H * N * S
BYTES = K * T + K * T // 32 + 4 * K * H + H * N + H * N // 32 + 2 * 4 * S + 2 * 2 * 128 * (S // 16) + 4 * N * S

F32 = mybir.dt.float32
BF16 = mybir.dt.bfloat16
I32 = mybir.dt.int32
U32 = mybir.dt.uint32
U16 = mybir.dt.uint16
U8 = mybir.dt.uint8
FP8X4 = mybir.dt.float8_e4m3fn_x4
MULT = mybir.AluOpType.mult
ADD = mybir.AluOpType.add
MAX = mybir.AluOpType.max
MIN = mybir.AluOpType.min
SUB = mybir.AluOpType.subtract
IS_GE = mybir.AluOpType.is_ge
COPY = mybir.ActivationFunctionType.Copy
ABS = mybir.ActivationFunctionType.Abs

P = 128
HALF = 512
BLOCKS = S // P
TILES = H // P
X_PIECES = [(0, 512), (512, 256), (768, 256)]
X_LAST = X_PIECES[2][0]
W_LOADS = [(0, 128), (128, 256), (256, 512)]
UNITS = [(0, 1), (2, 3), (6, 7), (4,), (5,)]
PAIR = 2 * P
RATIO = 6
MIXED = range(RATIO, BLOCKS)


def tile_picked_mixup_none_p_kernel(
    tc, x_words, x_scales, w1, w2_words, w2_scales, lam, mu, offs, pos1, out
):
    nc = tc.nc
    with ExitStack() as ctx:
        keep = ctx.enter_context(tc.tile_pool(name="keep", bufs=1))
        head = ctx.enter_context(tc.tile_pool(name="head", bufs=1))
        psum = ctx.enter_context(tc.psum_pool(name="psum", bufs=1))

        def bank(b):
            return psum.tile([P, HALF], F32, name="bank%d" % b, tag="bank%d" % b)

        def block_bank(b):
            return bank([0, 1, 2, 3, 5, 6, 7, 4][b])

        def tile(name, shape, dtype, tag=None):
            return keep.tile(shape, dtype, name=name, tag=tag or name, align_bytes=64)

        def entries(lst, j0, n):
            return lst[:, j0 // 16 : (j0 + n) // 16]

        def turn(dst_bank, t, src, start, stop):
            dst = dst_bank[:].rearrange("p (u t x) -> p u t x", u=2, t=TILES)[:, :, t, :]
            nc.tensor.matmul(dst, src, ident[:], start=start, stop=stop, is_transpose=True)

        offs_sb = keep.tile([P, S // 16], U16, name="offs_sb")
        pos_sb = keep.tile([P, S // 16], U16, name="pos_sb")
        xs = tile("xs", [P, T], U8)
        xw = tile("xw", [P, T], I32)
        shares = head.tile([P, P], F32, name="shares", offset=S - 256, align_bytes=64)
        w2w = tile("w2w", [P, N], I32)
        w2s = tile("w2s", [P, N], U8)
        ident = tile("ident", [P, P], F32)

        nc.gpsimd.memset(shares[:], 0.0)
        nc.vector.memset(xs[:].bitcast(I32), 0)
        nc.vector.memset(w2s[:].bitcast(I32), 0)
        nc.vector.memset(ident[:], 0.0)
        make_identity(nc, ident[:], nomemset=True)

        nc.sync.dma_start(shares[0:BLOCKS, :], lam[0, :].rearrange("(b c) -> b c", c=P))
        nc.sync.dma_start(shares[BLOCKS : 2 * BLOCKS, :], mu[0, :].rearrange("(b c) -> b c", c=P))
        nc.sync.dma_start(offs_sb[:], offs)
        for q in range(4):
            nc.sync.dma_start(xs[32 * q : 32 * q + 4, :].bitcast(I32), x_scales[0, 4 * q : 4 * q + 4, :].bitcast(I32))
        nc.sync.dma_start(xw[:], x_words[0].rearrange("p n t -> p (n t)").bitcast(I32))
        w_raw = []
        for c0, c1 in W_LOADS:
            raw = tile("w_raw%d" % c0, [P, 4, c1 - c0], F32)
            nc.sync.dma_start(raw[:], w1[:, c0:c1].rearrange("(p j) c -> p j c", j=4))
            for c in range(0, c1 - c0, P):
                w_raw.append(raw[:, :, c : c + P].rearrange("p j (q u e) -> p q j u e", u=2, e=2))
        nc.sync.dma_start(pos_sb[:], pos1)
        nc.sync.dma_start(w2w[:], w2_words[0].rearrange("p n t -> p (n t)").bitcast(I32))
        for q in range(4):
            nc.sync.dma_start(w2s[32 * q : 32 * q + 4, :].bitcast(I32), w2_scales[0, 4 * q : 4 * q + 4, :].bitcast(I32))

        turned = bank(2)
        nc.tensor.transpose(turned[:, 0:P], shares[:], ident[:])
        lam_mu = tile("lam_mu", [P, 2 * BLOCKS], F32)
        inverse = tile("inverse", [P, RATIO], F32)
        bounded = tile("bounded", [P, RATIO], F32)
        outer = tile("outer", [P, RATIO], F32)
        ratio = tile("ratio", [P, RATIO], F32, tag="w_grouped0")
        nc.vector.reciprocal(inverse[:], turned[:, 0:RATIO])
        nc.scalar.copy(lam_mu[:], turned[:, 0 : 2 * BLOCKS])
        floor = tile("floor", [P, RATIO], F32)
        nc.scalar.activation(floor[:], turned[:, BLOCKS : BLOCKS + RATIO], ABS, scale=2.0**-41)
        quotient = tile("quotient", [P, RATIO], F32)
        nc.gpsimd.tensor_scalar(bounded[:], inverse[:], -(2.0**120), 2.0**120, MAX, MIN)
        nc.gpsimd.tensor_tensor(quotient[:], lam_mu[:, BLOCKS : BLOCKS + RATIO], bounded[:], MULT)
        nc.gpsimd.tensor_scalar(ratio[:], quotient[:], -(2.0**40), 2.0**40, MAX, MIN)

        side = tile("side", [P, RATIO], F32)
        half_size = tile("half_size", [P, RATIO], F32)
        excess = tile("excess", [P, RATIO], F32)
        above = tile("above", [P, RATIO], F32)
        larger = tile("larger", [P, RATIO], F32)
        twice_size = tile("twice_size", [P, RATIO], F32)
        nc.gpsimd.tensor_scalar(side[:], inverse[:], 0.0, 0.5, IS_GE, SUB)
        nc.gpsimd.tensor_tensor(half_size[:], lam_mu[:, 0:RATIO], side[:], MULT)
        nc.gpsimd.tensor_tensor(excess[:], half_size[:], floor[:], SUB)
        nc.gpsimd.tensor_scalar(above[:], excess[:], 0.0, 1.0, MAX, MULT)
        nc.gpsimd.tensor_tensor(larger[:], floor[:], above[:], ADD)
        nc.gpsimd.tensor_scalar(twice_size[:], larger[:], 2.0**-121, 4.0, MAX, MULT)
        nc.gpsimd.tensor_tensor(outer[:], twice_size[:], side[:], MULT)

        xgs = head.tile([P, S], U8, name="xgs", offset=0, align_bytes=64)
        nc.vector.tensor_copy(xgs[:], xs[:].indirect(offs_sb[:]))

        rows = tile("rows", [P, RATIO * P], F32)
        for b0, n, b in ((0, 4, 0), (4, RATIO - 4, 1)):
            acc = bank(b)
            for k in range(n):
                col = ratio[:, b0 + k : b0 + k + 1].to_broadcast([P, P])
                nc.tensor.matmul(acc[:, k * P : (k + 1) * P], col, ident[:], start=True, stop=True, is_transpose=True)
            nc.scalar.copy(rows[:, b0 * P : (b0 + n) * P], acc[:, 0 : n * P])

        w_codes = tile("w_codes", [P, H], U32)
        w_scales = tile("w_scales", [P, H], U8)

        def round_w(t, grouped):
            copy = nc.scalar.copy if t < 2 else nc.vector.tensor_copy
            copy(grouped.rearrange("p u q e j -> p q j u e"), w_raw[t])

        def quantise_w(t, grouped):
            n = grouped.shape[1] * P
            nc.vector.quantize_mx(
                out=w_codes[:, t * P : t * P + n].bitcast(FP8X4),
                scales=w_scales[:, t * P : t * P + n],
                in_=grouped[:].rearrange("p t u q e j -> p (t u q e j)"),
            )

        w_grouped = [tile("w_grouped%d" % t, [P, 1, 2, 32, 2, 4], BF16, tag=["w_grouped0", "w_raw0"][t]) for t in range(2)]
        for t in range(2):
            round_w(t, w_grouped[t][:, 0])
        quantise_w(0, w_grouped[0])
        xg = head.tile([P, X_LAST], U32, name="xg", offset=S, align_bytes=64)
        xg_last = tile("xg_last", [P, S - X_LAST], U32, tag="w_grouped0")

        def picked(j0, n):
            return xg[:, j0 : j0 + n] if j0 < X_LAST else xg_last[:, j0 - X_LAST : j0 - X_LAST + n]

        for j0, n in ((0, X_LAST), (X_LAST, S - X_LAST)):
            nc.vector.tensor_copy(picked(j0, n), xw[:].bitcast(U32).indirect(entries(offs_sb, j0, n)))
        quantise_w(1, w_grouped[1])
        w_last = tile("w_last", [P, 2, 2, 32, 2, 4], BF16, tag="xw")
        for t in (2, 3):
            round_w(t, w_last[:, t - 2])

        def first_product(t, b, pieces, copy):
            acc = bank(b)
            j_first = pieces[0][0]
            for j0, n in pieces:
                nc.tensor.matmul_mx(
                    out=acc[:, j0 - j_first : j0 - j_first + n],
                    lhsT=w_codes[:, t * P : (t + 1) * P].bitcast(FP8X4),
                    lhsT_scale=w_scales[:, t * P : (t + 1) * P],
                    rhs=picked(j0, n).bitcast(FP8X4),
                    rhs_scale=xgs[:, j0 : j0 + n],
                    start=True,
                    stop=True,
                )
            width = sum(n for j0, n in pieces)
            copy(h[t][:, j_first : j_first + width], acc[:, 0:width])

        h = [tile("h%d" % t, [P, S], F32) for t in range(TILES)]
        first_product(0, 4, X_PIECES[0:1], nc.scalar.copy)
        first_product(0, 5, X_PIECES[1:2], nc.vector.tensor_copy)
        first_product(0, 6, X_PIECES[2:3], nc.scalar.copy)
        quantise_w(2, w_last)
        for t in range(1, TILES):
            first_product(t, 4 + (2 * t + 1) % 4, X_PIECES[0:1], nc.scalar.copy)
            first_product(t, 4 + (2 * t + 2) % 4, X_PIECES[1:3], nc.scalar.copy)

        banks = [block_bank(b) for b in range(BLOCKS)]
        mixed_own = {}
        for b in MIXED:
            nc.tensor.matmul_mx(
                out=banks[b][:],
                lhsT=picked(b * P, P).bitcast(FP8X4),
                lhsT_scale=xgs[:, b * P : (b + 1) * P],
                rhs=w_codes[:].bitcast(FP8X4),
                rhs_scale=w_scales[:],
                start=True,
                stop=True,
            )
            mixed_own[b] = tile("mixed_own%d" % b, [P, H], F32)
            nc.scalar.activation(
                mixed_own[b][:].rearrange("p (u t x) -> p u t x", u=2, t=TILES),
                banks[b][:].rearrange("p (t u x) -> p u t x", u=2, t=TILES),
                COPY,
                scale=lam_mu[:, b : b + 1],
            )
            banks[b] = block_bank(b)
        for t in range(TILES):
            for b in range(RATIO):
                turn(banks[b], t, h[t][:, b * P : (b + 1) * P], t == 0, False)
            n = 4
            dst = tile("partner%d" % t, [P, n * P], F32)
            nc.vector.tensor_tensor(dst[:], h[t][:].indirect(entries(pos_sb, 0, n * P)), rows[:, 0 : n * P], MULT)
            for b in range(n):
                turn(banks[b], t, dst[:, b * P : (b + 1) * P], False, t == TILES - 1)

        n_late = (RATIO - 4) * P
        n_mixed = len(MIXED) * P
        late = tile("partner_late", [P, TILES, n_late], F32, tag="w_grouped0")
        for t in range(TILES):
            dst = tile("partner_mixed%d" % t, [P, n_mixed], F32)
            if t == TILES - 1:
                nc.vector.tensor_copy(dst[:, 0:P], h[t][:].indirect(entries(pos_sb, RATIO * P, P)))
                nc.scalar.activation(dst[:, P:PAIR], h[t][:].indirect(entries(pos_sb, RATIO * P + P, P)), COPY)
            else:
                nc.scalar.activation(dst[:], h[t][:].indirect(entries(pos_sb, RATIO * P, n_mixed)), COPY)
            for k, b in enumerate(MIXED):
                turn(banks[b], t, dst[:, k * P : (k + 1) * P], True, True)

        z_turned = {}
        z_grouped = {}

        def round_block(b, on_vector=False):
            z = tile("z%d" % b, [P, H], BF16)
            if on_vector:
                nc.vector.tensor_scalar(z[:], banks[b][:], outer[:, b : b + 1], None, MULT)
            else:
                nc.scalar.activation(z[:], banks[b][:], COPY, scale=outer[:, b : b + 1])
            z_turned[b] = z

        def mix(b):
            z = tile("z%d" % b, [P, H], BF16)
            nc.vector.scalar_tensor_tensor(z[:], banks[b][:], lam_mu[:, BLOCKS + b : BLOCKS + b + 1], mixed_own[b][:], MULT, ADD)
            z_turned[b] = z

        backs = {}

        def turn_back(b):
            backs[b] = block_bank(b)
            words = z_turned[b][:].bitcast(F32)
            for u in range(2):
                nc.tensor.transpose(backs[b][:, u * P : (u + 1) * P], words[:, u * P : (u + 1) * P], ident[:])

        def group(unit):
            z_grouped[unit] = tile("z_grouped%d" % unit[0], [P, len(unit) * P, 2], F32)
            for k, b in enumerate(unit):
                nc.scalar.copy(
                    z_grouped[unit][:, k * P : (k + 1) * P, :], backs[b][:, 0 : 2 * P].rearrange("p (u j) -> p j u", u=2)
                )

        z_codes = tile("z_codes", [P, S], U32)

        sums = {}

        def second_product(unit):
            j0, n = unit[0] * P, len(unit) * P
            z_scales = tile("z_scales%d" % unit[0], [P, n], U8)
            nc.vector.quantize_mx(
                out=z_codes[:, j0 : j0 + n].bitcast(FP8X4),
                scales=z_scales[:],
                in_=z_grouped[unit][:].rearrange("p j u -> p (j u)").bitcast(BF16),
            )
            acc = block_bank(unit[-1])
            nc.tensor.matmul_mx(
                out=acc[:, 0:n],
                lhsT=w2w[:].bitcast(FP8X4),
                lhsT_scale=w2s[:],
                rhs=z_codes[:, j0 : j0 + n].bitcast(FP8X4),
                rhs_scale=z_scales[:],
                start=True,
                stop=True,
            )
            sums[unit] = acc

        def store(unit, copy):
            j0, n = unit[0] * P, len(unit) * P
            res = tile("res%d" % unit[0], [P, n], F32)
            copy(res[:], sums[unit][:, 0:n])
            nc.sync.dma_start(out[:, j0 : j0 + n], res[:])

        def late_partner(t):
            nc.vector.tensor_tensor(late[:, t, :], h[t][:].indirect(entries(pos_sb, HALF, n_late)), rows[:, HALF:], MULT)
            for b in range(4, RATIO):
                turn(banks[b], t, late[:, t, (b - 4) * P : (b - 3) * P], False, t == TILES - 1)

        late_partner(0)
        late_partner(1)
        for b in range(4):
            round_block(b)
        turn_back(0)
        late_partner(2)
        turn_back(1)
        late_partner(3)
        turn_back(2)
        turn_back(3)
        mix(6)
        mix(7)
        group(UNITS[0])
        group(UNITS[1])
        round_block(4, on_vector=True)
        round_block(5, on_vector=True)
        for unit in UNITS[2:]:
            for b in unit:
                turn_back(b)
            group(unit)
        for unit in UNITS:
            second_product(unit)
        for unit in UNITS:
            store(unit, nc.vector.tensor_copy if len(unit) == 1 else nc.scalar.copy)
